import numpy as np, ml_dtypes
CORES = [21,85,149,213,277,341,405,469]
N = 8
T, KB = 2048, 1024
CAPP = 512
def entries(a): return a.T.reshape(-1)
def pack(v, P): return np.ascontiguousarray(np.asarray(v, np.int32).reshape(-1, P).T)
def order(K):
    return np.argsort(K, kind="stable")
def most(K):
    o = order(K); return int(np.bincount(o // T * N + np.arange(N * T) // T, minlength=N * N).max())
def lists(rng, how):
    i, G = np.arange(N), T // CAPP
    if how == "uniform":
        for again in range(50):
            K = rng.integers(0, KB, (N, T))
            if most(K.reshape(-1)) <= CAPP: break
        else: K = np.broadcast_to(np.arange(T) % KB, (N, T)).copy()
    else:
        if how == "uneven":
            t = rng.integers(0, CAPP + 1, N)
            if t.sum() < T: t = CAPP - t
            t[0] = CAPP; w = np.diff(np.minimum(np.cumsum(t), T), prepend=0); L = w[(rng.permutation(N)[:, None] - rng.permutation(N)) % N]
        else:
            w = np.zeros(N, int); w[(G * (ord(how[-1]) - 97) + np.arange(G)) % N] = CAPP; L = w[(i[:, None] - i) % N]
        a = N - 1 - np.argmax(L[::-1] > 0, axis=0)
        m = np.minimum(rng.integers(1, CAPP, N - 1), L[a[:-1], i[1:]])
        v = np.nonzero((L[a[:-1], i[:-1]] == CAPP) & (L[a[:-1], i[1:]] == CAPP) & (a[:-1] != np.append(-1, a[:-2])))[0]
        if len(v): m[rng.choice(v)] = CAPP
        C = L.copy(); C[a[:-1], i[:-1]] += m; C[a[:-1], i[1:]] -= m
        kv = np.sort(rng.permutation(KB)[:N]); K = np.stack([rng.permutation(np.repeat(kv, c)) for c in C]); K[::3] = np.sort(K[::3], axis=1)
    return {"key": np.stack([pack(k, 16) for k in K])}
def setup_inputs(rng):
    return dict({"x": rng.standard_normal((N, 128, T), dtype=np.float32).astype(ml_dtypes.bfloat16)}, **lists(rng, "uniform"))
def setup_inputs_fulla(rng):
    d = setup_inputs(rng); d.update(lists(rng, "fulla"))
    for k in ("x",): d[k] = (d[k].astype(np.float32) * 1048576.0).astype(d[k].dtype)
    return d
def setup_inputs_fullb(rng):
    d = setup_inputs(rng); d.update(lists(rng, "fullb"))
    for k in ("x",): d[k] = (d[k].astype(np.float32) * (1 / 1024.0)).astype(d[k].dtype)
    return d
def setup_inputs_uneven(rng):
    d = setup_inputs(rng); d.update(lists(rng, "uneven"))
    return d
def check_inputs(x):
    bad = []
    if x["key"].min() < 0 or x["key"].max() >= KB: bad.append("key out of range")
    if most(np.concatenate([entries(a) for a in x["key"]])) > CAPP: bad.append("more than CAPP columns go from one rank to one rank")
    return bad
def reference(x, key):
    X = np.concatenate(list(x), axis=1); K = np.concatenate([entries(a) for a in key])
    Y = X[:, order(K)]
    return {"y": np.stack([Y[:, T * r:T * r + T] for r in range(N)])}

@@ -1,0 +1,365 @@
+from concourse.bass import DstId, RemoteDMATransfer
+from concourse.mybir import AluOpType as OP, ActivationFunctionType as AF
+
+N, TC, CAPP, NT = 8, 2048, 512, 16
+CORES_ALL = 512
+OPT = {
+    "seq": "W0 W1 X0 W2 X1 X2 C o",
+    "vg": (1,),
+    "xv": 512,
+}
+SCRATCH = {}
+
+
+def _buf(dtype, rows, **cols):
+    for k, n in cols.items():
+        SCRATCH[k] = ("sbuf", [rows, n], dtype)
+
+
+_buf("int32", 16, kI=128, hl32=256)
+_buf("bfloat16", 16, aHL=256, zsel=240)
+_buf("float32", 16, onesf=128, TLE=128, TGT=128, E=132)
+_buf("int32", 128, pI=128, sI=48, gp=216)
+_buf("uint16", 128, invl=128, off=256, yl=128)
+_buf("float16", 128, rs=1, HA=128, St=144, RB=2048, Zr=56, q3=72, LS=1024, RS=8192)
+_buf("bfloat16", 128, ones=512, iot=128, iom=128, ident=128, U4=512, LE=144, OH=2048, OHlo=128, OHT=2048, Mm=2048, rm8=128, rm9=72,
+     LA=2048, xin=2048, xs=2560, stage=4096, land=4096, yout=2048)
+_buf("float32", 128, jcol=16, b16=128, list0=128, lin=32, Dd=7, prod=128, SC=128, abf=32, HT=72, G9=72, Z=56, w32=504, gab=144, yl32=128)
+for _k in range(2):
+    SCRATCH["pT%d" % _k] = ("psum", [128, 1024], "bfloat16")
+for _k in range(6):
+    SCRATCH["f%d" % _k] = ("psum", [128, 512], "float32")
+SEMAPHORES = ["h1", "h2", "dat", "rel0", "rel1", "sent"] + ["e%d" % _k for _k in range(140)]
+
+
+def lp(r):
+    return 2 * r if r < N // 2 else 2 * N - 1 - 2 * r
+
+
+def chip_of(c, topo):
+    return [x for x in range(CORES_ALL) if topo.host(x) == topo.host(c) and topo.chip(x) == topo.chip(c)]
+
+
+def plan(T, topo):
+    cores = [int(c) for c in T.cores]
+    inr = {r: [s for s in range(N) if s != r and topo.rack(topo.host(cores[s])) == topo.rack(topo.host(cores[r]))] for r in range(N)}
+    cab = {r: [s for s in range(N) if s != r and s not in inr[r] and topo.may_write(cores[r], cores[s])
+               and topo.chip(cores[s]) == topo.chip(cores[r])][0] for r in range(N)}
+    W, X, role = {}, {}, {}
+    for q in range(N):
+        L = chip_of(cores[q], topo)
+        wl = [L[i] for i in range(0, len(L), 2) if cores[q] not in L[i:i + 2]]
+        for s, w in zip(inr[q], wl):
+            W[(s, cab[q])] = w
+            role.setdefault(w, []).append((s, cab[q], 0))
+        xl = [x for x in L if topo.die(x) != topo.die(cores[q]) and x not in wl]
+        for i, d in enumerate(inr[q]):
+            x, k = xl[i % len(xl)], i // len(xl)
+            X[(q, d)] = (x, k)
+            role.setdefault(x, []).append((q, d, k))
+    return cores, inr, cab, W, X, role
+
+
+def program(g, T):
+    Q = {"G": g, "V": g.vector, "S": g.scalar, "P": g.tensor, "Y": g.sync}
+    ops, cur, known, order = [], {}, {q: set() for q in Q}, []
+
+    def gen(q, ext=None, total=0):
+        x = {"n": len(order), "q": q, "open": True, "readers": [], "waited": ext is not None, "sem": ext, "total": total, "known": set()}
+        order.append(x)
+        return x
+
+    def external(key, sem, total):
+        cur[key] = gen(None, sem, total)
+        cur[key]["open"] = False
+
+    def op(q, fn, w, r=(), inc=1):
+        need = [cur[k] for k in r]
+        old = cur.get(w)
+        if old is not None and old["open"] and old["q"] == q and w not in r:
+            me = old
+        else:
+            if old is not None:
+                need += [old] + old["readers"]
+            me = gen(q)
+        waits = []
+        for x in sorted(need, key=lambda z: -z["n"]):
+            if x is me:
+                continue
+            x["open"] = False
+            if x["n"] not in known[q]:
+                x["waited"] = True
+                waits.append(x)
+                known[q].add(x["n"])
+                known[q] |= x["known"]
+        for k in r:
+            if me not in cur[k]["readers"]:
+                cur[k]["readers"].append(me)
+        cur[w] = me
+        me["total"] += inc
+        me["known"] |= known[q]
+        ops.append((q, fn, me, waits, inc))
+
+    def finish():
+        free = 0
+        for x in order:
+            if x["waited"] and x["sem"] is None:
+                x["sem"] = "e%d" % free
+                free += 1
+        for q, fn, me, waits, inc in ops:
+            for x in waits:
+                Q[q].wait_ge(T.sem[x["sem"]], x["total"])
+            ins = fn()
+            if me["waited"] and inc:
+                ins.then_inc(T.sem[me["sem"]], inc)
+
+    return op, external, finish
+
+
+def rank_program(g, core, T, topo):
+    cores, inr, cab, W, X, role = plan(T, topo)
+    r = T.rank_of(core)
+    if r is None:
+        if core in role:
+            helper(g, core, T, topo, role[core], cores)
+        return
+    V, S, P, Y = g.vector, g.scalar, g.tensor, g.sync
+    op, external, finish = program(g, T)
+    rack = [s for s in range(N) if s in inr[r] or s == r]
+    far = [s for s in range(N) if s not in rack]
+    external("h1", "h1", 8 * (len(rack) - 1))
+    external("h2", "h2", 8)
+    external("dat", "dat", 8 * (N - 1))
+
+    def mm(key, out, lhs, rhs, a, b, rd):
+        op("P", lambda: P.matmul(out, lhs, rhs, a, b), key, rd)
+
+    def ts(key, out, in0, s1, s2, o0, o1=None, rd=()):
+        if o1 is None:
+            op("V", lambda: V.tensor_scalar(out, in0, s1, None, o0), key, rd)
+        else:
+            op("V", lambda: V.tensor_scalar(out, in0, s1, s2, o0, o1), key, rd)
+
+    def tt(key, out, in0, in1, o, rd=()):
+        op("V", lambda: V.tensor_tensor(out, in0, in1, o), key, rd)
+
+    def scan(key, out, d0, d1, init, rd):
+        op("V", lambda: V.tensor_tensor_scan(out, d0, d1, init, OP.mult, OP.add), key, rd)
+
+    def cp(key, out, in_, rd=()):
+        op("V", lambda: V.tensor_copy(out, in_), key, rd)
+
+    def act(key, out, in_, rd=()):
+        op("S", lambda: S.activation(out, in_, AF.Copy), key, rd)
+
+    def ms(key, ap, v, rd=()):
+        op("V", lambda: V.memset(ap, v), key, rd)
+
+    def dma(key, out, in_, rd=()):
+        op("Y", lambda: Y.dma_start(out, in_), key, rd, 16)
+
+    def iota(key, ap, pat, base, cm):
+        op("G", lambda: g.iota(ap, pat, base, cm, allow_small_or_imprecise_dtypes=True), key)
+
+    def aff(key, ap, in_, pat, cmp, base, cm, rd):
+        op("G", lambda: g.affine_select(ap, in_, pat, cmp, 0.0, base, cm), key, rd)
+
+    def w32(i, a=0, b=72):
+        return T.w32[:, 72 * i + a:72 * i + b]
+
+    def tile(buf, t, n=128):
+        return T[buf][:, n * t:n * t + n]
+
+    dma("kI", T.kI[:], T.key[:])
+    dma("xin", T.xin[:], T.x[:])
+    ms("ones", T.ones[:], 1.0)
+    aff("zsel", T.zsel[:], T.ones[0:16, 0:240], [[1, 240]], OP.is_equal, -112, -1, ["ones"])
+    iota("iot", T.iot[:], [[1, 128]], 0, 0)
+    aff("U4", T.U4[:], T.ones[:], [[0, 4], [1, 128]], OP.is_gt, 0, -1, ["ones"])
+    aff("ident", T.ident[:], T.ones[:, 0:128], [[1, 128]], OP.is_equal, 0, -1, ["ones"])
+    iota("iom", T.iom[:], [[0, 8], [1, 16]], 0, 0)
+    iota("jcol", T.jcol[:], [[128, 16]], 0, 1)
+    iota("pI", T.pI[:], [[0, 128]], 0, 1)
+    iota("Dd", T.Dd[:], [[TC, 7]], TC, 0)
+    ms("LEc", T.LE[:, 0::9], 0.0)
+    ms("LEc", T.LE[:, 8::9], 1.0)
+    ms("rm8a", T.rm8[:], 1.0)
+    ms("rm9a", T.rm9[:], 1.0)
+    ms("hpad", tile("HA", r, 16), 0.0)
+    ms("xpad", T.xs[:, TC:TC + CAPP], 0.0)
+
+    ts("hl32", T.hl32[:, 0:128], T.kI[:], 3, None, OP.arith_shift_right, rd=["kI"])
+    ts("hl32", T.hl32[:, 128:256], T.kI[:], 7, None, OP.bitwise_and, rd=["kI"])
+    cp("aHL", T.aHL[:], T.hl32[:], ["hl32"])
+    ms("rm8", T.rm8[:, 0::8], 0.0, ["rm8a"])
+    ms("rm9", T.rm9[:, 0::9], 0.0, ["rm9a"])
+    ms("onesf", T.onesf[:], 1.0)
+    for u in range(8):
+        mm("f0", T.f0[:, 0:32], T.zsel[:, 112 - 16 * u:240 - 16 * u], T.aHL[:, u::8], u == 0, u == 7, ["zsel", "aHL"])
+    for i in range(1, 8):
+        ts("LE", T.LE[:, i::9], T.f0[:, 16:32], float(i), None, OP.is_lt, rd=["f0"])
+    for t in range(NT):
+        ts("OH%d" % (t // 4), tile("OH", t), T.iot[:], T.f0[:, t:t + 1], None, OP.is_equal, rd=["f0", "iot"])
+    for t in range(NT):
+        mm("f1", T.f1[:, 0:9], tile("OH", t), tile("LE", t, 9), t == 0, t == NT - 1, ["OH%d" % (t // 4), "LE", "LEc"])
+    cp("rs", T.rs[:], T.f1[:, 8:9], ["f1"])
+
+    def transpose(t):
+        out = tile("pT%d" % (t // 8), t % 8)
+        op("P", lambda: P.transpose(out, tile("OH", t), T.ident[:]), "pT%d" % (t // 8), ["OH%d" % (t // 4), "ident"])
+    for t in range(2):
+        transpose(t)
+    mm("f3", T.f3[:, 0:1], T.U4[:, 0:128], T.rs[:], True, True, ["U4", "rs"])
+    for t in range(2, NT):
+        transpose(t)
+    ts("A", T.HA[:, 16 * r:16 * r + 9], T.f1[:, 0:9], T.f3[:, 0:1], None, OP.add, rd=["f1", "f3", "hpad"])
+
+    own = tile("HA", r, 16)
+    sent = [0]
+
+    def send_counts():
+        ds = [DstId(rid=topo.addr(cores[s], core)[0], pnc=topo.addr(cores[s], core)[1]) for s in inr[r]]
+        return g.remote_dma_fused([RemoteDMATransfer(dst_ids=ds, srcs=[own], dsts=[own for s in ds], alu_op=0,
+                                                     dma_engine_mask=topo.mask(core, cores[inr[r][0]]), remote_sem=T.sem.h1)],
+                                  local_sem=T.sem.sent)
+
+    def remote(key, rd, out, in_, dst, sem, mask):
+        rid, pid = topo.addr(dst, core)
+        op("G", lambda: g.remote_dma(out, in_, T.sem[sem], T.sem.sent, pid, rid, mask), key, rd, 0)
+        sent[0] += 8
+    op("G", send_counts, "s0", ["A"], 0)
+    sent[0] += 8
+    blk = T.HA[:, 16 * rack[0]:16 * rack[0] + 16 * len(rack)]
+    remote("s1", ["A", "h1"], blk, blk, cores[cab[r]], "h2", topo.mask(core, cores[cab[r]]))
+    iota("b16", T.b16[:], [[16, 128]], 0, 0)
+    aff("TLE", T.TLE[:], T.onesf[:], [[0, 8], [1, 16]], OP.is_ge, 0, -1, ["onesf"])
+    aff("TGT", T.TGT[:], T.onesf[:], [[0, 8], [-1, 16]], OP.is_gt, 0, 1, ["onesf"])
+
+    for l in range(8):
+        ts("OHlo", T.OHlo[:, l::8], T.f0[:, 16:32], float(l), None, OP.is_equal, rd=["f0"])
+    for t in range(NT):
+        mm("f2", T.f2[:, t:128:16], tile("OH", t), tile("OHlo", t, 8), True, True, ["OH%d" % (t // 4), "OHlo"])
+    act("OHT0", T.OHT[:, 0:1024], T.pT0[:], ["pT0"])
+    ts("pm", T.pI[:], T.pI[:], 15, None, OP.bitwise_and, rd=["pI"])
+    ms("E0", T.E[:, 0:4], 0.0)
+    for s in range(N):
+        ms("Jc", w32(6, 9 * s, 9 * s + 9), float(CAPP * (lp(s) - lp((s - 1) % N))))
+    cp("OHT1", T.OHT[:, 1024:2048], T.pT1[:], ["pT1"])
+    cp("St0", T.St[:, 0:1], T.f3[:, 0:1], ["f3"])
+    scan("St", T.St[:, 1:129], T.ones[:, 0:128], T.f2[:, 0:128], T.f3[:, 0:1], ["f2", "f3", "ones"])
+    mb = ["f4", "f5", "f1", "f0"]
+    for t in range(NT):
+        mm(mb[t // 4], tile(mb[t // 4], t % 4), tile("OHT", t), tile("OHT", t), True, True, ["OHT%d" % (t // 8)])
+    for k in range(4):
+        tt("Mm%d" % k, tile("Mm", k, 512), T[mb[k]][:], T.U4[:], OP.mult, [mb[k], "U4"])
+    for t in range(NT):
+        o = tile("f2", t, 8)
+        mm("f2", o, tile("OHT", t), T.St[:, t:128:16], True, False, ["OHT%d" % (t // 8), "St", "St0"])
+        mm("f2", o, tile("Mm", t), tile("OHlo", t, 8), False, True, ["Mm%d" % (t // 4), "OHlo"])
+    tt("prod", T.prod[:], T.f2[:, 0:128], T.OHlo[:], OP.mult, ["f2", "OHlo"])
+    scan("SC", T.SC[:], T.rm8[:], T.prod[:], 0.0, ["prod", "rm8"])
+    cp("sI", T.sI[:, 0:16], T.SC[:, 7::8], ["SC"])
+    ts("ab32", T.sI[:, 16:32], T.sI[:, 0:16], 15, None, OP.bitwise_and, rd=["sI"])
+    ts("ab32", T.sI[:, 32:48], T.sI[:, 0:16], 4, None, OP.arith_shift_right, rd=["sI"])
+    cp("abf", T.abf[:], T.sI[:, 16:48], ["ab32"])
+    for t in range(NT):
+        k = "LA%d" % (t // 4)
+        ts(k, tile("LA", t), T.iom[:], T.abf[:, t:t + 1], None, OP.is_equal, rd=["iom", "abf"])
+        ts(k, tile("RB", t), T.iot[:], T.abf[:, 16 + t:17 + t], T.jcol[:, t:t + 1], OP.is_equal, OP.mult, rd=["iot", "abf", "jcol"])
+    for t in range(NT):
+        mm("f4", T.f4[:, 0:128], tile("LA", t), tile("RB", t), t == 0, t == NT - 1, ["LA%d" % (t // 4)])
+
+    def src_key(s):
+        return "A" if s == r else ("h1" if s in rack else "h2")
+
+    def lengths(ss):
+        for s in ss:
+            tt("HT", T.HT[:, 1 + s::9], T.HA[:, 16 * s + 1:16 * s + 9], T.HA[:, 16 * s:16 * s + 8], OP.subtract, [src_key(s)])
+    lengths(rack)
+    cp("invl", T.invl[:], T.f4[:, 0:128], ["f4"])
+    H = OPT["xv"]
+    act("xsS", T.xs[:, H:TC], T.xin[:].indirect(T.invl[:, H // 16:128]), ["xin", "invl"])
+    lengths(far)
+    for i, s in enumerate(rack + far):
+        mm("f5", T.f5[:, 0:8], T.ident[:], T.HA[:, 16 * s:16 * s + 8], i == 0, i == N - 1, ["ident", src_key(s)])
+    cp("HT0", T.HT[:, 0::9], T.f5[:, 0:8], ["f5"])
+    scan("G9", T.G9[:], T.rm9[:], T.HT[:], 0.0, ["HT", "HT0", "rm9"])
+    for l in range(8):
+        e = 9 * l + r
+        ts("Z", tile("Z", l, 7), T.Dd[:], T.G9[:, e:e + 1], T.HT[:, e + 1:e + 2], OP.subtract, OP.min, rd=["Dd", "G9", "HT"])
+    ts("Zr", T.Zr[:], T.Z[:], 0.0, None, OP.max, rd=["Z"])
+    for l in range(8):
+        mm("f1", T.f1[:, 0:7], T.ones[:, 0:128], tile("Zr", l, 7), l == 0, l == 7, ["ones", "Zr"])
+    cp("xsV", T.xs[:, 0:H], T.xin[:].indirect(T.invl[:, 0:H // 16]), ["xin", "invl"])
+    tt("lin", T.lin[:], T.b16[:, 0:32], T.pI[:, 0:32], OP.add, ["b16", "pm"])
+    seq = []
+    for z in OPT["seq"].split():
+        k = int(z[1:]) if z[1:] else 0
+        seq.append({"W": ("W", cab[inr[r][k]]), "X": ("X", inr[r][k]), "C": ("C", cab[r]), "o": ("own", r)}[z[0]])
+    for how, d in seq:
+        if d == 0:
+            cp("off%d" % d, tile("off", d, 32), T.lin[:], ["lin"])
+        else:
+            ts("off%d" % d, tile("off", d, 32), T.lin[:], T.f1[:, d - 1:d], None, OP.add, rd=["lin", "f1"])
+
+    for i, (how, d) in enumerate(seq):
+        out = tile("land", lp(r), CAPP) if how == "own" else tile("stage", d, CAPP)
+        (cp if i in OPT["vg"] else act)("st%d" % d, out, T.xs[:].indirect(tile("off", d, 32)), ["xsS", "xsV", "xpad", "off%d" % d])
+    for how, d in seq:
+        src, key, rd = tile("stage", d, CAPP), "s_%d" % d, ["st%d" % d]
+        if how == "W":
+            remote(key, rd, tile("land", 0, CAPP), src, W[(r, d)], "rel0", topo.mask(core, W[(r, d)]))
+        elif how == "X":
+            x, k = X[(r, d)]
+            m = topo.mask(core, x) & ~topo.mask(core, cores[d])
+            remote(key, rd, tile("land", k, CAPP), src, x, "rel%d" % k, m)
+        elif how == "C":
+            remote(key, rd, tile("land", lp(r), CAPP), src, cores[d], "dat", topo.mask(core, cores[d]))
+
+    ts("q1", w32(0), T.G9[:], -1.0, float(TC * r), OP.mult, OP.add, rd=["G9"])
+    tt("q2", w32(1, 0, 71), w32(0, 0, 71), T.HT[:, 1:72], OP.min, ["q1", "HT", "HT0"])
+    ts("q3", T.q3[:, 0:71], w32(1, 0, 71), 0.0, None, OP.max, rd=["q2"])
+    for l in range(8):
+        mm("f3", T.f3[:, 0:8], T.ones[:, 0:128], T.q3[:, 9 * l:9 * l + 8], l == 0, l == 7, ["ones", "q3"])
+    ts("gp", T.gp[:, 144:216], T.G9[:], float(TC * r), 0.0, OP.subtract, OP.max, rd=["G9"])
+    ts("gab32", T.gp[:, 72:144], T.gp[:, 144:216], 4, None, OP.arith_shift_right, rd=["gp"])
+    ts("gab32", T.gp[:, 0:72], T.gp[:, 144:216], 15, None, OP.bitwise_and, rd=["gp"])
+    cp("gab", T.gab[:], T.gp[:, 0:144], ["gab32"])
+    tt("list0a", T.list0[:], T.b16[:], T.pI[:], OP.add, ["b16", "pm"])
+    for s in range(N):
+        ts("a1", w32(2, 9 * s, 9 * s + 9), T.HA[:, 16 * s:16 * s + 9], T.f3[:, s:s + 1], 0.0, OP.subtract, OP.max, rd=["f3", "h1", "h2", "A"])
+    ts("a2", w32(3), w32(2), float(CAPP), None, OP.min, rd=["a1"])
+    ts("list0", T.list0[:], T.list0[:], float(CAPP * lp(N - 1)), None, OP.add, rd=["list0a"])
+    tt("dl", w32(4, 9, 72), w32(3, 9, 72), w32(3, 1, 64), OP.subtract, ["a2"])
+    tt("dl", w32(4, 0, 8), w32(3, 0, 8), w32(3, 63, 71), OP.subtract, ["a2"])
+    ms("dl", w32(4, 8, 9), 0.0)
+    tt("dl2", w32(5), w32(4), w32(6), OP.add, ["dl", "Jc"])
+    for i in range(64):
+        l, s = i // N, i % N
+        e, k = 9 * l + s, "sg%d" % (i // 4)
+        ts(k, tile("RS", i), T.iot[:], T.gab[:, 72 + e:73 + e], None, OP.is_equal, rd=["iot", "gab"])
+        ts(k, tile("LS", i, 16), T.iot[:, 0:16], T.gab[:, e:e + 1], w32(5, 9 * s + l, 9 * s + l + 1), OP.is_equal, OP.mult,
+           rd=["iot", "gab", "dl2"])
+    for i in range(64):
+        mm("f4", T.f4[0:16, 0:128], tile("LS", i, 16), tile("RS", i), i == 0, i == 63, ["sg%d" % (i // 4)])
+    scan("E", T.E[:, 4:132], T.onesf[:], T.f4[0:16, 0:128], 0.0, ["f4", "onesf"])
+    mm("f2", T.f2[:, 0:128], T.TLE[:], T.E[:, 4:132], True, False, ["TLE", "E"])
+    mm("f2", T.f2[:, 0:128], T.TGT[:], T.E[:, 3:131], False, True, ["TGT", "E", "E0"])
+    tt("yl32", T.yl32[:], T.f2[:, 0:128], T.list0[:], OP.add, ["f2", "list0"])
+    cp("yl", T.yl[:], T.yl32[:], ["yl32"])
+    for c in range(4):
+        (cp if c % 2 == 0 else act)("y%d" % c, tile("yout", c, 512), T.land[:].indirect(tile("yl", c, 32)), ["yl", "dat", "st%d" % r])
+    for c in range(4):
+        dma("yo", tile("y", c, 512), tile("yout", c, 512), ["y%d" % c])
+    op("Y", lambda: None, "end", ["yo"], 0)
+    finish()
+    g.wait_ge(T.sem.sent, sent[0])
+
+
+def helper(g, core, T, topo, jobs, cores):
+    for s, d, k in jobs:
+        rid, pid = topo.addr(cores[d], core)
+        g.wait_ge(T.sem["rel%d" % k], 8)
+        g.remote_dma(T.land[:, CAPP * lp(s):CAPP * lp(s) + CAPP], T.land[:, CAPP * k:CAPP * k + CAPP], T.sem.dat, T.sem.sent,
+                     pid, rid, topo.mask(core, cores[d]))
+    g.wait_ge(T.sem.sent, 8 * len(jobs))

@@ -3,11 +3,9 @@ from concourse.mybir import AluOpType as OP, ActivationFunctionType as AF
 
 N, TC, CAPP, NT = 8, 2048, 512, 16
 CORES_ALL = 512
-OPT = {
-    "seq": "W0 W1 X0 W2 X1 X2 C o",
-    "vg": (1,),
-    "xv": 512,
-}
+C0 = 64
+R8, R16 = 1.5 * 2 ** 26, 1.5 * 2 ** 27
+YC = (0, 640, 1280, 1664, 2048)
 SCRATCH = {}
 
 
@@ -16,20 +14,21 @@ def _buf(dtype, rows, **cols):
         SCRATCH[k] = ("sbuf", [rows, n], dtype)
 
 
-_buf("int32", 16, kI=128, hl32=256)
-_buf("bfloat16", 16, aHL=256, zsel=240)
-_buf("float32", 16, onesf=128, TLE=128, TGT=128, E=132)
-_buf("int32", 128, pI=128, sI=48, gp=216)
-_buf("uint16", 128, invl=128, off=256, yl=128)
-_buf("float16", 128, rs=1, HA=128, St=144, RB=2048, Zr=56, q3=72, LS=1024, RS=8192)
-_buf("bfloat16", 128, ones=512, iot=128, iom=128, ident=128, U4=512, LE=144, OH=2048, OHlo=128, OHT=2048, Mm=2048, rm8=128, rm9=72,
-     LA=2048, xin=2048, xs=2560, stage=4096, land=4096, yout=2048)
-_buf("float32", 128, jcol=16, b16=128, list0=128, lin=32, Dd=7, prod=128, SC=128, abf=32, HT=72, G9=72, Z=56, w32=504, gab=144, yl32=128)
+_buf("int32", 16, kI=128)
+_buf("bfloat16", 16, zsel=240)
+_buf("float16", 16, kF=128)
+_buf("int32", 128, pI=32, gp=216)
+_buf("uint16", 128, invl=128, off=256, yl=128, rep=8)
+_buf("float16", 128, HA=128, Ex=144, St=144, RB=2048, Zr=56, q3=72, LS=1152, RS=8192)
+_buf("bfloat16", 128, ones=512, iot=128, iot8=128, iot16=128, iom=128, ident=128, U4=512, OH=2048, OHlo=128, OHT=2048, Mm=2048,
+     rm8=128, rm9=72, LA=2048, xin=2048, xs=2560, stage=4096, land=4096, yout=2048, ga=72)
+_buf("float32", 128, jcol=16, hi=48, b16=32, lin=32, Dd=7, prod=128, SC=128, abf=32, HT=72, G9=72, Z=56, w32=504, gb=72,
+     id32=128, U32=128, E=16, Er=128, Rr=128, pa=1)
 for _k in range(2):
     SCRATCH["pT%d" % _k] = ("psum", [128, 1024], "bfloat16")
 for _k in range(6):
     SCRATCH["f%d" % _k] = ("psum", [128, 512], "float32")
-SEMAPHORES = ["h1", "h2", "dat", "rel0", "rel1", "sent"] + ["e%d" % _k for _k in range(140)]
+SEMAPHORES = ["h1", "h2", "dat", "relw", "rel0", "rel1", "sent"] + ["e%d" % _k for _k in range(143)]
 
 
 def lp(r):
@@ -42,8 +41,9 @@ def chip_of(c, topo):
 
 def plan(T, topo):
     cores = [int(c) for c in T.cores]
-    inr = {r: [s for s in range(N) if s != r and topo.rack(topo.host(cores[s])) == topo.rack(topo.host(cores[r]))] for r in range(N)}
-    cab = {r: [s for s in range(N) if s != r and s not in inr[r] and topo.may_write(cores[r], cores[s])
+    racks = {r: [s for s in range(N) if topo.rack(topo.host(cores[s])) == topo.rack(topo.host(cores[r]))] for r in range(N)}
+    inr = {r: sorted([s for s in racks[r] if s != r], key=lambda s: (s - r) % len(racks[r])) for r in range(N)}
+    cab = {r: [s for s in range(N) if s not in racks[r] and topo.may_write(cores[r], cores[s])
                and topo.chip(cores[s]) == topo.chip(cores[r])][0] for r in range(N)}
     W, X, role = {}, {}, {}
     for q in range(N):
@@ -51,13 +51,15 @@ def plan(T, topo):
         wl = [L[i] for i in range(0, len(L), 2) if cores[q] not in L[i:i + 2]]
         for s, w in zip(inr[q], wl):
             W[(s, cab[q])] = w
-            role.setdefault(w, []).append((s, cab[q], 0))
+            cut = (0, C0, CAPP) if inr[s].index(q) else (0, CAPP)
+            role.setdefault(w, []).extend((s, cab[q], 0, a, b) for a, b in zip(cut, cut[1:]))
         xl = [x for x in L if topo.die(x) != topo.die(cores[q]) and x not in wl]
         for i, d in enumerate(inr[q]):
             x, k = xl[i % len(xl)], i // len(xl)
             X[(q, d)] = (x, k)
-            role.setdefault(x, []).append((q, d, k))
-    return cores, inr, cab, W, X, role
+            cut = (0, CAPP) if k else (0, C0, CAPP)
+            role.setdefault(x, []).extend((q, d, k, a, b) for a, b in zip(cut, cut[1:]))
+    return cores, racks, inr, cab, W, X, role
 
 
 def program(g, T):
@@ -117,7 +119,7 @@ def program(g, T):
 
 
 def rank_program(g, core, T, topo):
-    cores, inr, cab, W, X, role = plan(T, topo)
+    cores, racks, inr, cab, W, X, role = plan(T, topo)
     r = T.rank_of(core)
     if r is None:
         if core in role:
@@ -125,11 +127,11 @@ def rank_program(g, core, T, topo):
         return
     V, S, P, Y = g.vector, g.scalar, g.tensor, g.sync
     op, external, finish = program(g, T)
-    rack = [s for s in range(N) if s in inr[r] or s == r]
+    rack = racks[r]
     far = [s for s in range(N) if s not in rack]
     external("h1", "h1", 8 * (len(rack) - 1))
     external("h2", "h2", 8)
-    external("dat", "dat", 8 * (N - 1))
+    external("dat", "dat", 8 * (N - 1) + 8 * 2 * (len(rack) - 2))
 
     def mm(key, out, lhs, rhs, a, b, rd):
         op("P", lambda: P.matmul(out, lhs, rhs, a, b), key, rd)
@@ -174,45 +176,53 @@ def rank_program(g, core, T, topo):
     dma("xin", T.xin[:], T.x[:])
     ms("ones", T.ones[:], 1.0)
     aff("zsel", T.zsel[:], T.ones[0:16, 0:240], [[1, 240]], OP.is_equal, -112, -1, ["ones"])
-    iota("iot", T.iot[:], [[1, 128]], 0, 0)
-    aff("U4", T.U4[:], T.ones[:], [[0, 4], [1, 128]], OP.is_gt, 0, -1, ["ones"])
+    iota("iot8", T.iot8[:], [[8, 128]], 0, 0)
     aff("ident", T.ident[:], T.ones[:, 0:128], [[1, 128]], OP.is_equal, 0, -1, ["ones"])
+    aff("U4", T.U4[:], T.ones[:], [[0, 4], [1, 128]], OP.is_gt, 0, -1, ["ones"])
     iota("iom", T.iom[:], [[0, 8], [1, 16]], 0, 0)
+    iota("iot16", T.iot16[:], [[16, 128]], 0, 0)
     iota("jcol", T.jcol[:], [[128, 16]], 0, 1)
-    iota("pI", T.pI[:], [[0, 128]], 0, 1)
+    iota("pI", T.pI[:], [[0, 32]], 0, 1)
+    iota("b16", T.b16[:], [[16, 32]], 0, 0)
+    iota("iot", T.iot[:], [[1, 128]], 0, 0)
     iota("Dd", T.Dd[:], [[TC, 7]], TC, 0)
-    ms("LEc", T.LE[:, 0::9], 0.0)
-    ms("LEc", T.LE[:, 8::9], 1.0)
     ms("rm8a", T.rm8[:], 1.0)
     ms("rm9a", T.rm9[:], 1.0)
     ms("hpad", tile("HA", r, 16), 0.0)
     ms("xpad", T.xs[:, TC:TC + CAPP], 0.0)
+    ms("Ex0", T.Ex[:, 0:1], 0.0)
 
-    ts("hl32", T.hl32[:, 0:128], T.kI[:], 3, None, OP.arith_shift_right, rd=["kI"])
-    ts("hl32", T.hl32[:, 128:256], T.kI[:], 7, None, OP.bitwise_and, rd=["kI"])
-    cp("aHL", T.aHL[:], T.hl32[:], ["hl32"])
+    cp("kF", T.kF[:], T.kI[:], ["kI"])
     ms("rm8", T.rm8[:, 0::8], 0.0, ["rm8a"])
     ms("rm9", T.rm9[:, 0::9], 0.0, ["rm9a"])
-    ms("onesf", T.onesf[:], 1.0)
     for u in range(8):
-        mm("f0", T.f0[:, 0:32], T.zsel[:, 112 - 16 * u:240 - 16 * u], T.aHL[:, u::8], u == 0, u == 7, ["zsel", "aHL"])
-    for i in range(1, 8):
-        ts("LE", T.LE[:, i::9], T.f0[:, 16:32], float(i), None, OP.is_lt, rd=["f0"])
+        mm("f0", T.f0[:, 0:16], T.zsel[:, 112 - 16 * u:240 - 16 * u], T.kF[:, u::8], u == 0, u == 7, ["zsel", "kF"])
+    ts("hi1", T.hi[:, 0:16], T.f0[:, 0:16], -3.5, R8, OP.add, OP.add, rd=["f0"])
+    ts("hi8", T.hi[:, 16:32], T.hi[:, 0:16], -R8, None, OP.add, rd=["hi1"])
+    tt("lo", T.hi[:, 32:48], T.f0[:, 0:16], T.hi[:, 16:32], OP.subtract, ["f0", "hi8"])
+
+    def onehot_hi(t):
+        ts("OH%d" % (t // 4), tile("OH", t), T.iot8[:], T.hi[:, 16 + t:17 + t], None, OP.is_equal, rd=["hi8", "iot8"])
+    for t in range(4):
+        onehot_hi(t)
+    for l in range(8):
+        ts("OHlo", T.OHlo[:, l::8], T.hi[:, 32:48], float(l), None, OP.is_equal, rd=["lo"])
+    for t in range(4, NT):
+        onehot_hi(t)
     for t in range(NT):
-        ts("OH%d" % (t // 4), tile("OH", t), T.iot[:], T.f0[:, t:t + 1], None, OP.is_equal, rd=["f0", "iot"])
-    for t in range(NT):
-        mm("f1", T.f1[:, 0:9], tile("OH", t), tile("LE", t, 9), t == 0, t == NT - 1, ["OH%d" % (t // 4), "LE", "LEc"])
-    cp("rs", T.rs[:], T.f1[:, 8:9], ["f1"])
+        mm("f2", T.f2[:, t:128:16], tile("OH", t), tile("OHlo", t, 8), True, True, ["OH%d" % (t // 4), "OHlo"])
+    scan("Ex", T.Ex[:, 1:129], T.ones[:, 0:128], T.f2[:, 0:128], 0.0, ["f2", "ones"])
 
     def transpose(t):
         out = tile("pT%d" % (t // 8), t % 8)
         op("P", lambda: P.transpose(out, tile("OH", t), T.ident[:]), "pT%d" % (t // 8), ["OH%d" % (t // 4), "ident"])
     for t in range(2):
         transpose(t)
-    mm("f3", T.f3[:, 0:1], T.U4[:, 0:128], T.rs[:], True, True, ["U4", "rs"])
+    mm("f3", T.f3[:, 0:1], T.U4[:, 0:128], T.Ex[:, 128:129], True, True, ["U4", "Ex"])
     for t in range(2, NT):
         transpose(t)
-    ts("A", T.HA[:, 16 * r:16 * r + 9], T.f1[:, 0:9], T.f3[:, 0:1], None, OP.add, rd=["f1", "f3", "hpad"])
+    ts("A", T.HA[:, 16 * r:16 * r + 9], T.Ex[:, 0:129:16], T.f3[:, 0:1], None, OP.add, rd=["Ex", "Ex0", "f3", "hpad"])
+    ts("St", T.St[:, 0:129], T.Ex[:, 0:129], T.f3[:, 0:1], None, OP.add, rd=["Ex", "Ex0", "f3"])
 
     own = tile("HA", r, 16)
     sent = [0]
@@ -222,52 +232,50 @@ def rank_program(g, core, T, topo):
         return g.remote_dma_fused([RemoteDMATransfer(dst_ids=ds, srcs=[own], dsts=[own for s in ds], alu_op=0,
                                                      dma_engine_mask=topo.mask(core, cores[inr[r][0]]), remote_sem=T.sem.h1)],
                                   local_sem=T.sem.sent)
-
-    def remote(key, rd, out, in_, dst, sem, mask):
-        rid, pid = topo.addr(dst, core)
-        op("G", lambda: g.remote_dma(out, in_, T.sem[sem], T.sem.sent, pid, rid, mask), key, rd, 0)
-        sent[0] += 8
     op("G", send_counts, "s0", ["A"], 0)
-    sent[0] += 8
     blk = T.HA[:, 16 * rack[0]:16 * rack[0] + 16 * len(rack)]
-    remote("s1", ["A", "h1"], blk, blk, cores[cab[r]], "h2", topo.mask(core, cores[cab[r]]))
-    iota("b16", T.b16[:], [[16, 128]], 0, 0)
-    aff("TLE", T.TLE[:], T.onesf[:], [[0, 8], [1, 16]], OP.is_ge, 0, -1, ["onesf"])
-    aff("TGT", T.TGT[:], T.onesf[:], [[0, 8], [-1, 16]], OP.is_gt, 0, 1, ["onesf"])
+    rid_c, pid_c = topo.addr(cores[cab[r]], core)
+    op("G", lambda: g.remote_dma(blk, blk, T.sem.h2, T.sem.sent, pid_c, rid_c, topo.mask(core, cores[cab[r]])), "s1", ["A", "h1"], 0)
+    sent[0] += 16
 
-    for l in range(8):
-        ts("OHlo", T.OHlo[:, l::8], T.f0[:, 16:32], float(l), None, OP.is_equal, rd=["f0"])
-    for t in range(NT):
-        mm("f2", T.f2[:, t:128:16], tile("OH", t), tile("OHlo", t, 8), True, True, ["OH%d" % (t // 4), "OHlo"])
     act("OHT0", T.OHT[:, 0:1024], T.pT0[:], ["pT0"])
     ts("pm", T.pI[:], T.pI[:], 15, None, OP.bitwise_and, rd=["pI"])
-    ms("E0", T.E[:, 0:4], 0.0)
+    tt("lin", T.lin[:], T.b16[:], T.pI[:], OP.add, ["b16", "pm"])
+    cp("rep", T.rep[:], T.pI[:, 0:8], ["pm"])
+    ts("pa", T.pa[:], T.pI[:, 0:1], float(CAPP * lp(N - 1)), None, OP.add, rd=["pm"])
+    cp("id32", T.id32[:], T.ident[:], ["ident"])
+    cp("U32", T.U32[:], T.U4[:, 0:128], ["U4"])
     for s in range(N):
         ms("Jc", w32(6, 9 * s, 9 * s + 9), float(CAPP * (lp(s) - lp((s - 1) % N))))
     cp("OHT1", T.OHT[:, 1024:2048], T.pT1[:], ["pT1"])
-    cp("St0", T.St[:, 0:1], T.f3[:, 0:1], ["f3"])
-    scan("St", T.St[:, 1:129], T.ones[:, 0:128], T.f2[:, 0:128], T.f3[:, 0:1], ["f2", "f3", "ones"])
     mb = ["f4", "f5", "f1", "f0"]
-    for t in range(NT):
-        mm(mb[t // 4], tile(mb[t // 4], t % 4), tile("OHT", t), tile("OHT", t), True, True, ["OHT%d" % (t // 8)])
-    for k in range(4):
+
+    def equal_hi(k):
+        for t in range(4 * k, 4 * k + 4):
+            mm(mb[k], tile(mb[k], t % 4), tile("OHT", t), tile("OHT", t), True, True, ["OHT%d" % (t // 8)])
         tt("Mm%d" % k, tile("Mm", k, 512), T[mb[k]][:], T.U4[:], OP.mult, [mb[k], "U4"])
-    for t in range(NT):
-        o = tile("f2", t, 8)
-        mm("f2", o, tile("OHT", t), T.St[:, t:128:16], True, False, ["OHT%d" % (t // 8), "St", "St0"])
-        mm("f2", o, tile("Mm", t), tile("OHlo", t, 8), False, True, ["Mm%d" % (t // 4), "OHlo"])
+
+    def places(k):
+        for t in range(4 * k, 4 * k + 4):
+            o = tile("f2", t, 8)
+            mm("f2", o, tile("OHT", t), T.St[:, t:128:16], True, False, ["OHT%d" % (t // 8), "St"])
+            mm("f2", o, tile("Mm", t), tile("OHlo", t, 8), False, True, ["Mm%d" % k, "OHlo"])
+    for k in range(3):
+        equal_hi(k)
+    places(0)
+    equal_hi(3)
+    for k in range(1, 4):
+        places(k)
     tt("prod", T.prod[:], T.f2[:, 0:128], T.OHlo[:], OP.mult, ["f2", "OHlo"])
     scan("SC", T.SC[:], T.rm8[:], T.prod[:], 0.0, ["prod", "rm8"])
-    cp("sI", T.sI[:, 0:16], T.SC[:, 7::8], ["SC"])
-    ts("ab32", T.sI[:, 16:32], T.sI[:, 0:16], 15, None, OP.bitwise_and, rd=["sI"])
-    ts("ab32", T.sI[:, 32:48], T.sI[:, 0:16], 4, None, OP.arith_shift_right, rd=["sI"])
-    cp("abf", T.abf[:], T.sI[:, 16:48], ["ab32"])
+    ts("b1", T.abf[:, 0:16], T.SC[:, 7::8], -7.5, R16, OP.add, OP.add, rd=["SC"])
+    ts("b0", T.abf[:, 16:32], T.abf[:, 0:16], -R16, None, OP.add, rd=["b1"])
     for t in range(NT):
-        k = "LA%d" % (t // 4)
-        ts(k, tile("LA", t), T.iom[:], T.abf[:, t:t + 1], None, OP.is_equal, rd=["iom", "abf"])
-        ts(k, tile("RB", t), T.iot[:], T.abf[:, 16 + t:17 + t], T.jcol[:, t:t + 1], OP.is_equal, OP.mult, rd=["iot", "abf", "jcol"])
+        k, b = "LA%d" % (t // 2), T.abf[:, 16 + t:17 + t]
+        ts(k, tile("LA", t), T.iom[:], b, T.SC[:, 8 * t + 7:8 * t + 8], OP.add, OP.is_equal, rd=["iom", "b0", "SC"])
+        ts(k, tile("RB", t), T.iot16[:], b, T.jcol[:, t:t + 1], OP.is_equal, OP.mult, rd=["iot16", "b0", "jcol"])
     for t in range(NT):
-        mm("f4", T.f4[:, 0:128], tile("LA", t), tile("RB", t), t == 0, t == NT - 1, ["LA%d" % (t // 4)])
+        mm("f4", T.f4[:, 0:128], tile("LA", t), tile("RB", t), t == 0, t == NT - 1, ["LA%d" % (t // 2)])
 
     def src_key(s):
         return "A" if s == r else ("h1" if s in rack else "h2")
@@ -277,7 +285,7 @@ def rank_program(g, core, T, topo):
             tt("HT", T.HT[:, 1 + s::9], T.HA[:, 16 * s + 1:16 * s + 9], T.HA[:, 16 * s:16 * s + 8], OP.subtract, [src_key(s)])
     lengths(rack)
     cp("invl", T.invl[:], T.f4[:, 0:128], ["f4"])
-    H = OPT["xv"]
+    H = 512
     act("xsS", T.xs[:, H:TC], T.xin[:].indirect(T.invl[:, H // 16:128]), ["xin", "invl"])
     lengths(far)
     for i, s in enumerate(rack + far):
@@ -291,75 +299,106 @@ def rank_program(g, core, T, topo):
     for l in range(8):
         mm("f1", T.f1[:, 0:7], T.ones[:, 0:128], tile("Zr", l, 7), l == 0, l == 7, ["ones", "Zr"])
     cp("xsV", T.xs[:, 0:H], T.xin[:].indirect(T.invl[:, 0:H // 16]), ["xin", "invl"])
-    tt("lin", T.lin[:], T.b16[:, 0:32], T.pI[:, 0:32], OP.add, ["b16", "pm"])
-    seq = []
-    for z in OPT["seq"].split():
-        k = int(z[1:]) if z[1:] else 0
-        seq.append({"W": ("W", cab[inr[r][k]]), "X": ("X", inr[r][k]), "C": ("C", cab[r]), "o": ("own", r)}[z[0]])
-    for how, d in seq:
+    peers = inr[r]
+    via = {}
+    for q in peers:
+        w, (x, k) = W[(r, cab[q])], X[(r, q)]
+        via[cab[q]] = (w, "rel0", topo.mask(core, w), 0)
+        via[q] = (x, "rel%d" % k, topo.mask(core, x) & ~topo.mask(core, cores[q]), CAPP * k)
+    via[cab[r]] = (cores[cab[r]], "dat", topo.mask(core, cores[cab[r]]), CAPP * lp(r))
+    w0, w1, w2 = [cab[q] for q in peers]
+    x0, x1, x2 = peers
+    c = cab[r]
+    for d in (w0, w1, x0, w2, x1, x2, c, r):
         if d == 0:
             cp("off%d" % d, tile("off", d, 32), T.lin[:], ["lin"])
         else:
             ts("off%d" % d, tile("off", d, 32), T.lin[:], T.f1[:, d - 1:d], None, OP.add, rd=["lin", "f1"])
 
-    for i, (how, d) in enumerate(seq):
-        out = tile("land", lp(r), CAPP) if how == "own" else tile("stage", d, CAPP)
-        (cp if i in OPT["vg"] else act)("st%d" % d, out, T.xs[:].indirect(tile("off", d, 32)), ["xsS", "xsV", "xpad", "off%d" % d])
-    for how, d in seq:
-        src, key, rd = tile("stage", d, CAPP), "s_%d" % d, ["st%d" % d]
-        if how == "W":
-            remote(key, rd, tile("land", 0, CAPP), src, W[(r, d)], "rel0", topo.mask(core, W[(r, d)]))
-        elif how == "X":
-            x, k = X[(r, d)]
-            m = topo.mask(core, x) & ~topo.mask(core, cores[d])
-            remote(key, rd, tile("land", k, CAPP), src, x, "rel%d" % k, m)
-        elif how == "C":
-            remote(key, rd, tile("land", lp(r), CAPP), src, cores[d], "dat", topo.mask(core, cores[d]))
+    def gather(f, d, a=0, b=CAPP):
+        o = CAPP * lp(r) if d == r else CAPP * d
+        f("st%d_%d" % (d, a), T["land" if d == r else "stage"][:, o + a:o + b], T.xs[:].indirect(T.off[:, 32 * d + a // 16:32 * d + b // 16]),
+          ["xsS", "xsV", "xpad", "off%d" % d])
+
+    def half(m, i):
+        e = [b for b in range(m.bit_length()) if m >> b & 1]
+        return sum(1 << b for b in e[i * len(e) // 2:(i + 1) * len(e) // 2])
+
+    def ship(*blocks):
+        trs = []
+        for d, a, b, sem, m in blocks:
+            to, s0, m0, o = via[d]
+            rid, pid = topo.addr(to, core)
+            trs.append(RemoteDMATransfer(dst_ids=[DstId(rid=rid, pnc=pid)], srcs=[T.stage[:, CAPP * d + a:CAPP * d + b]],
+                                         dsts=[T.land[:, o + a:o + b]], alu_op=0, dma_engine_mask=m or m0, remote_sem=T.sem[sem or s0]))
+            sent[0] += bin(m or m0).count("1")
+        op("G", lambda: g.remote_dma_fused(trs, local_sem=T.sem.sent), "s_%d_%d" % blocks[0][:2], ["st%d_%d" % b[:2] for b in blocks], 0)
+
+    def rest(d):
+        return (d, C0, CAPP, None, None)
+    early = (w1, x0, w2, x1)
+    gather(act, w0)
+    for d in early:
+        gather(act, d, 0, C0)
+    for f, d in ((cp, w1), (act, x0), (cp, w2), (act, x1)):
+        gather(f, d, C0)
+    for d in (x2, c, r):
+        gather(act, d)
+    ship((w0, 0, CAPP, None, None))
+    ship(*[(d, 0, C0, "relw", half(via[d][2], i // 2)) for i, d in enumerate(early)])
+    ship(rest(w1), rest(x0))
+    ship(rest(w2), rest(x1))
+    ship((x2, 0, CAPP, None, None), (c, 0, CAPP, None, None))
 
     ts("q1", w32(0), T.G9[:], -1.0, float(TC * r), OP.mult, OP.add, rd=["G9"])
+    ts("gp", T.gp[:, 144:216], T.G9[:], float(TC * r), 0.0, OP.subtract, OP.max, rd=["G9"])
     tt("q2", w32(1, 0, 71), w32(0, 0, 71), T.HT[:, 1:72], OP.min, ["q1", "HT", "HT0"])
+    ts("gab32", T.gp[:, 72:144], T.gp[:, 144:216], 4, None, OP.arith_shift_right, rd=["gp"])
+    ts("gab32", T.gp[:, 0:72], T.gp[:, 144:216], 15, None, OP.bitwise_and, rd=["gp"])
     ts("q3", T.q3[:, 0:71], w32(1, 0, 71), 0.0, None, OP.max, rd=["q2"])
     for l in range(8):
         mm("f3", T.f3[:, 0:8], T.ones[:, 0:128], T.q3[:, 9 * l:9 * l + 8], l == 0, l == 7, ["ones", "q3"])
-    ts("gp", T.gp[:, 144:216], T.G9[:], float(TC * r), 0.0, OP.subtract, OP.max, rd=["G9"])
-    ts("gab32", T.gp[:, 72:144], T.gp[:, 144:216], 4, None, OP.arith_shift_right, rd=["gp"])
-    ts("gab32", T.gp[:, 0:72], T.gp[:, 144:216], 15, None, OP.bitwise_and, rd=["gp"])
-    cp("gab", T.gab[:], T.gp[:, 0:144], ["gab32"])
-    tt("list0a", T.list0[:], T.b16[:], T.pI[:], OP.add, ["b16", "pm"])
+    cp("ga", T.ga[:], T.gp[:, 0:72], ["gab32"])
+    cp("gb", T.gb[:], T.gp[:, 72:144], ["gab32"])
+    for a in range(16):
+        ts("LS", T.LS[:, a::16], T.ga[:], float(a), None, OP.is_equal, rd=["ga"])
     for s in range(N):
         ts("a1", w32(2, 9 * s, 9 * s + 9), T.HA[:, 16 * s:16 * s + 9], T.f3[:, s:s + 1], 0.0, OP.subtract, OP.max, rd=["f3", "h1", "h2", "A"])
     ts("a2", w32(3), w32(2), float(CAPP), None, OP.min, rd=["a1"])
-    ts("list0", T.list0[:], T.list0[:], float(CAPP * lp(N - 1)), None, OP.add, rd=["list0a"])
     tt("dl", w32(4, 9, 72), w32(3, 9, 72), w32(3, 1, 64), OP.subtract, ["a2"])
     tt("dl", w32(4, 0, 8), w32(3, 0, 8), w32(3, 63, 71), OP.subtract, ["a2"])
     ms("dl", w32(4, 8, 9), 0.0)
     tt("dl2", w32(5), w32(4), w32(6), OP.add, ["dl", "Jc"])
     for i in range(64):
         l, s = i // N, i % N
-        e, k = 9 * l + s, "sg%d" % (i // 4)
-        ts(k, tile("RS", i), T.iot[:], T.gab[:, 72 + e:73 + e], None, OP.is_equal, rd=["iot", "gab"])
-        ts(k, tile("LS", i, 16), T.iot[:, 0:16], T.gab[:, e:e + 1], w32(5, 9 * s + l, 9 * s + l + 1), OP.is_equal, OP.mult,
-           rd=["iot", "gab", "dl2"])
+        e = 9 * l + s
+        ts("sg%d" % (i // 4), tile("RS", i), T.iot[:], T.gb[:, e:e + 1], w32(5, 9 * s + l, 9 * s + l + 1), OP.is_equal, OP.mult,
+           rd=["iot", "gb", "dl2"])
     for i in range(64):
-        mm("f4", T.f4[0:16, 0:128], tile("LS", i, 16), tile("RS", i), i == 0, i == 63, ["sg%d" % (i // 4)])
-    scan("E", T.E[:, 4:132], T.onesf[:], T.f4[0:16, 0:128], 0.0, ["f4", "onesf"])
-    mm("f2", T.f2[:, 0:128], T.TLE[:], T.E[:, 4:132], True, False, ["TLE", "E"])
-    mm("f2", T.f2[:, 0:128], T.TGT[:], T.E[:, 3:131], False, True, ["TGT", "E", "E0"])
-    tt("yl32", T.yl32[:], T.f2[:, 0:128], T.list0[:], OP.add, ["f2", "list0"])
-    cp("yl", T.yl[:], T.yl32[:], ["yl32"])
-    for c in range(4):
-        (cp if c % 2 == 0 else act)("y%d" % c, tile("yout", c, 512), T.land[:].indirect(tile("yl", c, 32)), ["yl", "dat", "st%d" % r])
-    for c in range(4):
-        dma("yo", tile("y", c, 512), tile("yout", c, 512), ["y%d" % c])
+        mm("f4", T.f4[:, 0:16], tile("RS", i), tile("LS", 9 * (i // N) + i % N, 16), i == 0, i == 63, ["sg%d" % (i // 4), "LS"])
+    scan("E", T.E[:], T.ones[:, 0:16], T.f4[:, 0:16], 0.0, ["f4", "ones"])
+    ts("Rr", T.Rr[:], T.ones[:, 0:128], T.E[:, 15:16], 16.0, OP.mult, OP.add, rd=["E", "ones"])
+    mm("f2", T.f2[:, 0:128], T.Rr[:], T.U32[:], True, False, ["Rr", "U32"])
+    cp("Er", T.Er[:], T.E[:].indirect(T.rep[:]), ["E", "rep"])
+    mm("f2", T.f2[:, 0:128], T.Er[:], T.id32[:], False, True, ["Er", "id32"])
+    ts("yl", T.yl[:], T.f2[:, 0:128], T.pa[:], None, OP.add, rd=["f2", "pa"])
+    for k in range(4):
+        (cp if k % 2 == 0 else act)("y%d" % k, T.yout[:, YC[k]:YC[k + 1]], T.land[:].indirect(T.yl[:, YC[k] // 16:YC[k + 1] // 16]),
+                                    ["yl", "dat", "st%d_0" % r])
+    for k in range(4):
+        dma("yo", T.y[:, YC[k]:YC[k + 1]], T.yout[:, YC[k]:YC[k + 1]], ["y%d" % k])
     op("Y", lambda: None, "end", ["yo"], 0)
     finish()
     g.wait_ge(T.sem.sent, sent[0])
 
 
 def helper(g, core, T, topo, jobs, cores):
-    for s, d, k in jobs:
+    for s, d, k, a, b in jobs:
         rid, pid = topo.addr(cores[d], core)
-        g.wait_ge(T.sem["rel%d" % k], 8)
-        g.remote_dma(T.land[:, CAPP * lp(s):CAPP * lp(s) + CAPP], T.land[:, CAPP * k:CAPP * k + CAPP], T.sem.dat, T.sem.sent,
-                     pid, rid, topo.mask(core, cores[d]))
+        if b < CAPP:
+            g.wait_ge(T.sem.relw, 4)
+        else:
+            g.wait_ge(T.sem["rel%d" % k], 8)
+        o, i = CAPP * lp(s), CAPP * k
+        g.remote_dma(T.land[:, o + a:o + b], T.land[:, i + a:i + b], T.sem.dat, T.sem.sent, pid, rid, topo.mask(core, cores[d]))
     g.wait_ge(T.sem.sent, 8 * len(jobs))

@@ -4,8 +4,10 @@ from concourse.mybir import AluOpType as OP, ActivationFunctionType as AF
 N, TC, CAPP, NT = 8, 2048, 512, 16
 CORES_ALL = 512
 C0 = 64
+XA = 128
+H = 512
 R8, R16 = 1.5 * 2 ** 26, 1.5 * 2 ** 27
-YC = (0, 640, 1280, 1664, 2048)
+YC = (0, 512, 1024, 1536, 2048)
 SCRATCH = {}
 
 
@@ -20,15 +22,15 @@ _buf("float16", 16, kF=128)
 _buf("int32", 128, pI=32, gp=216)
 _buf("uint16", 128, invl=128, off=256, yl=128, rep=8)
 _buf("float16", 128, HA=128, Ex=144, St=144, RB=2048, Zr=56, q3=72, LS=1152, RS=8192)
-_buf("bfloat16", 128, ones=512, iot=128, iot8=128, iot16=128, iom=128, ident=128, U4=512, OH=2048, OHlo=128, OHT=2048, Mm=2048,
+_buf("bfloat16", 128, ones=512, iot8=128, cst=384, ident=128, U4=512, OH=2048, OHlo=128, OHT=2048, Mm=2048,
      rm8=128, rm9=72, LA=2048, xin=2048, xs=2560, stage=4096, land=4096, yout=2048, ga=72)
-_buf("float32", 128, jcol=16, hi=48, b16=32, lin=32, Dd=7, prod=128, SC=128, abf=32, HT=72, G9=72, Z=56, w32=504, gb=72,
-     id32=128, U32=128, E=16, Er=128, Rr=128, pa=1)
+_buf("float32", 128, cstf=192, hi=48, b16=32, prod=128, SC=128, abf=32, HT=72, G9=72, Z=56, w32=504, gb=72,
+     U32=128, E=16, Er=128, Rr=128)
 for _k in range(2):
     SCRATCH["pT%d" % _k] = ("psum", [128, 1024], "bfloat16")
 for _k in range(6):
     SCRATCH["f%d" % _k] = ("psum", [128, 512], "float32")
-SEMAPHORES = ["h1", "h2", "dat", "relw", "rel0", "rel1", "sent"] + ["e%d" % _k for _k in range(143)]
+SEMAPHORES = ["h1", "h2", "dat", "cs", "xd", "il", "yls", "relw", "rel", "sent"] + ["e%d" % _k for _k in range(138)]
 
 
 def lp(r):
@@ -45,21 +47,23 @@ def plan(T, topo):
     inr = {r: sorted([s for s in racks[r] if s != r], key=lambda s: (s - r) % len(racks[r])) for r in range(N)}
     cab = {r: [s for s in range(N) if s not in racks[r] and topo.may_write(cores[r], cores[s])
                and topo.chip(cores[s]) == topo.chip(cores[r])][0] for r in range(N)}
-    W, X, role = {}, {}, {}
+    W, X, Z, role, mine = {}, {}, {}, {}, {}
     for q in range(N):
         L = chip_of(cores[q], topo)
         wl = [L[i] for i in range(0, len(L), 2) if cores[q] not in L[i:i + 2]]
-        for s, w in zip(inr[q], wl):
-            W[(s, cab[q])] = w
-            cut = (0, C0, CAPP) if inr[s].index(q) else (0, CAPP)
-            role.setdefault(w, []).extend((s, cab[q], 0, a, b) for a, b in zip(cut, cut[1:]))
-        xl = [x for x in L if topo.die(x) != topo.die(cores[q]) and x not in wl]
-        for i, d in enumerate(inr[q]):
-            x, k = xl[i % len(xl)], i // len(xl)
-            X[(q, d)] = (x, k)
-            cut = (0, CAPP) if k else (0, C0, CAPP)
-            role.setdefault(x, []).extend((q, d, k, a, b) for a, b in zip(cut, cut[1:]))
-    return cores, racks, inr, cab, W, X, role
+        pairs = [(w, s, cab[q]) for s, w in zip(inr[q], wl)]
+        X[q] = [x for x in L if topo.die(x) != topo.die(cores[q]) and x not in wl][0]
+        spare = [x for x in L if x not in wl and x not in (cores[q], X[q])]
+        for x, d in ((X[q], inr[q][1]), (cores[q], inr[q][2])):
+            w = [w for w in spare if topo.die(w) == topo.die(x)][0]
+            pairs.append((w, q, d))
+            spare.remove(w)
+        Z[q] = spare[0]
+        mine[X[q]] = mine[Z[q]] = q
+        for w, s, d in pairs:
+            W[(s, d)] = w
+            role[w] = [(s, d, a, b) for a, b in ((0, C0), (C0, CAPP))]
+    return cores, racks, inr, cab, W, X, Z, role, mine
 
 
 def program(g, T):
@@ -118,20 +122,44 @@ def program(g, T):
     return op, external, finish
 
 
+def count_bits(m):
+    return bin(m).count("1")
+
+
+def half(m, i):
+    e = [b for b in range(m.bit_length()) if m >> b & 1]
+    return sum(1 << b for b in e[i * len(e) // 2:(i + 1) * len(e) // 2])
+
+
 def rank_program(g, core, T, topo):
-    cores, racks, inr, cab, W, X, role = plan(T, topo)
-    r = T.rank_of(core)
-    if r is None:
+    cores, racks, inr, cab, W, X, Z, role, mine = plan(T, topo)
+    own = T.rank_of(core) is not None
+    if not own and core not in mine:
         if core in role:
             helper(g, core, T, topo, role[core], cores)
         return
+    r = T.rank_of(core) if own else mine[core]
+    third = core == Z[r]
     V, S, P, Y = g.vector, g.scalar, g.tensor, g.sync
     op, external, finish = program(g, T)
     rack = racks[r]
     far = [s for s in range(N) if s not in rack]
-    external("h1", "h1", 8 * (len(rack) - 1))
-    external("h2", "h2", 8)
-    external("dat", "dat", 8 * (N - 1) + 8 * 2 * (len(rack) - 2))
+    c, other = cab[r], X[r] if own else cores[r]
+    off_chip = topo.mask(core, cores[inr[r][0]])
+    on_chip = topo.mask(core, other)
+    stay = on_chip & ~off_chip
+    sent = [0]
+    if own:
+        external("h1", "h1", 8 * (len(rack) - 1))
+        external("h2", "h2", 8)
+        external("cs", "cs", 2 * 8)
+        external("yl", "yls", 8)
+        external("dat", "dat", 8 * (N - 1) + 8 * sum((s, r) in W for s in range(N)))
+    else:
+        external("h2", "h2", 2 * 8)
+        if not third:
+            external("xin", "xd", count_bits(on_chip) + count_bits(stay))
+            external("invl", "il", count_bits(on_chip))
 
     def mm(key, out, lhs, rhs, a, b, rd):
         op("P", lambda: P.matmul(out, lhs, rhs, a, b), key, rd)
@@ -166,190 +194,242 @@ def rank_program(g, core, T, topo):
     def aff(key, ap, in_, pat, cmp, base, cm, rd):
         op("G", lambda: g.affine_select(ap, in_, pat, cmp, 0.0, base, cm), key, rd)
 
+    def send(name, rd, *trs):
+        def call():
+            L = []
+            for to, src, dst, m, sem in trs:
+                ad = [topo.addr(t, core) for t in to]
+                L.append(RemoteDMATransfer(dst_ids=[DstId(rid=i, pnc=p) for i, p in ad], srcs=[src], dsts=[dst for t in to], alu_op=0,
+                                           dma_engine_mask=m, remote_sem=T.sem[sem]))
+            return g.remote_dma_fused(L, local_sem=T.sem.sent)
+        sent[0] += sum(count_bits(tr[3]) for tr in trs)
+        op("G", call, name, rd, 0)
+
     def w32(i, a=0, b=72):
         return T.w32[:, 72 * i + a:72 * i + b]
 
     def tile(buf, t, n=128):
         return T[buf][:, n * t:n * t + n]
 
-    dma("kI", T.kI[:], T.key[:])
-    dma("xin", T.xin[:], T.x[:])
+    iom, iot16, iot = [tile("cst", i) for i in range(3)]
+    id32, jcol, lin, Dd, pa, pm8 = [T.cstf[:, i:j] for i, j in ((0, 128), (128, 144), (144, 176), (176, 183), (183, 184), (184, 192))]
+    if own:
+        dma("kI", T.kI[:], T.key[:])
+        dma("xa", T.xin[:, 0:XA], T.x[:, 0:XA])
+        dma("xin", T.xin[:, XA:TC], T.x[:, XA:TC])
     ms("ones", T.ones[:], 1.0)
-    aff("zsel", T.zsel[:], T.ones[0:16, 0:240], [[1, 240]], OP.is_equal, -112, -1, ["ones"])
-    iota("iot8", T.iot8[:], [[8, 128]], 0, 0)
-    aff("ident", T.ident[:], T.ones[:, 0:128], [[1, 128]], OP.is_equal, 0, -1, ["ones"])
-    aff("U4", T.U4[:], T.ones[:], [[0, 4], [1, 128]], OP.is_gt, 0, -1, ["ones"])
-    iota("iom", T.iom[:], [[0, 8], [1, 16]], 0, 0)
-    iota("iot16", T.iot16[:], [[16, 128]], 0, 0)
-    iota("jcol", T.jcol[:], [[128, 16]], 0, 1)
-    iota("pI", T.pI[:], [[0, 32]], 0, 1)
-    iota("b16", T.b16[:], [[16, 32]], 0, 0)
-    iota("iot", T.iot[:], [[1, 128]], 0, 0)
-    iota("Dd", T.Dd[:], [[TC, 7]], TC, 0)
-    ms("rm8a", T.rm8[:], 1.0)
     ms("rm9a", T.rm9[:], 1.0)
-    ms("hpad", tile("HA", r, 16), 0.0)
-    ms("xpad", T.xs[:, TC:TC + CAPP], 0.0)
-    ms("Ex0", T.Ex[:, 0:1], 0.0)
+    if not third:
+        ms("xpad", T.xs[:, TC:TC + CAPP], 0.0)
+    if own:
+        aff("zsel", T.zsel[:], T.ones[0:16, 0:240], [[1, 240]], OP.is_equal, -112, -1, ["ones"])
+        iota("iot8", T.iot8[:], [[8, 128]], 0, 0)
+        aff("ident", T.ident[:], T.ones[:, 0:128], [[1, 128]], OP.is_equal, 0, -1, ["ones"])
+        aff("U1", T.U4[:, 0:128], T.ones[:, 0:128], [[1, 128]], OP.is_gt, 0, -1, ["ones"])
+        send("sxa", ["xa"], ([other], T.xin[:, 0:XA], T.xin[:, 0:XA], on_chip, "xd"))
+        ms("rm8a", T.rm8[:], 1.0)
+        ms("hpad", tile("HA", r, 16), 0.0)
+        ms("Ex0", T.Ex[:, 0:1], 0.0)
+        ms("rm8", T.rm8[:, 0::8], 0.0, ["rm8a"])
+        ms("rm9", T.rm9[:, 0::9], 0.0, ["rm9a"])
+    else:
+        if third:
+            iota("cst", iom, [[0, 8], [1, 16]], 0, 0)
+            iota("cst", iot16, [[16, 128]], 0, 0)
+            iota("cst", iot, [[1, 128]], 0, 0)
+            send("scs", ["cst"], ([other], T.cst[:], T.cst[:], off_chip, "cs"))
+        iota("pI", T.pI[:], [[0, 32]], 0, 1)
+        iota("b16", T.b16[:], [[16, 32]], 0, 0)
+        aff("ident", T.ident[:], T.ones[:, 0:128], [[1, 128]], OP.is_equal, 0, -1, ["ones"])
+        ts("pm", T.pI[:], T.pI[:], 15, None, OP.bitwise_and, rd=["pI"])
+        cp("pm8", pm8, T.pI[:, 0:8], ["pm"])
+        ts("pa", pa, T.pI[:, 0:1], float(CAPP * lp(N - 1)), None, OP.add, rd=["pm"])
+        cp("id32", id32, T.ident[:], ["ident"])
+        ms("rm9", T.rm9[:, 0::9], 0.0, ["rm9a"])
+        if third:
+            aff("U1", T.U4[:, 0:128], T.ones[:, 0:128], [[1, 128]], OP.is_gt, 0, -1, ["ones"])
+            for s in range(N):
+                ms("Jc", w32(6, 9 * s, 9 * s + 9), float(CAPP * (lp(s) - lp((s - 1) % N))))
+            ms("dlz", w32(4, 8, 9), 0.0)
+            cp("rep", T.rep[:], T.pI[:, 0:8], ["pm"])
+            cp("U32", T.U32[:], T.U4[:, 0:128], ["U1"])
+        else:
+            iota("jcol", jcol, [[128, 16]], 0, 1)
+            iota("Dd", Dd, [[TC, 7]], TC, 0)
+            tt("lin", lin, T.b16[:], T.pI[:], OP.add, ["b16", "pm"])
+            send("scs", ["jcol", "Dd", "lin", "pm8", "pa", "id32"], ([other], T.cstf[:], T.cstf[:], off_chip, "cs"))
 
-    cp("kF", T.kF[:], T.kI[:], ["kI"])
-    ms("rm8", T.rm8[:, 0::8], 0.0, ["rm8a"])
-    ms("rm9", T.rm9[:, 0::9], 0.0, ["rm9a"])
-    for u in range(8):
-        mm("f0", T.f0[:, 0:16], T.zsel[:, 112 - 16 * u:240 - 16 * u], T.kF[:, u::8], u == 0, u == 7, ["zsel", "kF"])
-    ts("hi1", T.hi[:, 0:16], T.f0[:, 0:16], -3.5, R8, OP.add, OP.add, rd=["f0"])
-    ts("hi8", T.hi[:, 16:32], T.hi[:, 0:16], -R8, None, OP.add, rd=["hi1"])
-    tt("lo", T.hi[:, 32:48], T.f0[:, 0:16], T.hi[:, 16:32], OP.subtract, ["f0", "hi8"])
+    def kc(k):
+        return "cs" if own else k
 
-    def onehot_hi(t):
-        ts("OH%d" % (t // 4), tile("OH", t), T.iot8[:], T.hi[:, 16 + t:17 + t], None, OP.is_equal, rd=["hi8", "iot8"])
-    for t in range(4):
-        onehot_hi(t)
-    for l in range(8):
-        ts("OHlo", T.OHlo[:, l::8], T.hi[:, 32:48], float(l), None, OP.is_equal, rd=["lo"])
-    for t in range(4, NT):
-        onehot_hi(t)
-    for t in range(NT):
-        mm("f2", T.f2[:, t:128:16], tile("OH", t), tile("OHlo", t, 8), True, True, ["OH%d" % (t // 4), "OHlo"])
-    scan("Ex", T.Ex[:, 1:129], T.ones[:, 0:128], T.f2[:, 0:128], 0.0, ["f2", "ones"])
+    if own:
+        cp("kF", T.kF[:], T.kI[:], ["kI"])
+        for u in range(8):
+            mm("f0", T.f0[:, 0:16], T.zsel[:, 112 - 16 * u:240 - 16 * u], T.kF[:, u::8], u == 0, u == 7, ["zsel", "kF"])
+        ts("hi1", T.hi[:, 0:16], T.f0[:, 0:16], -3.5, R8, OP.add, OP.add, rd=["f0"])
+        ts("hi8", T.hi[:, 16:32], T.hi[:, 0:16], -R8, None, OP.add, rd=["hi1"])
+        tt("lo", T.hi[:, 32:48], T.f0[:, 0:16], T.hi[:, 16:32], OP.subtract, ["f0", "hi8"])
 
-    def transpose(t):
-        out = tile("pT%d" % (t // 8), t % 8)
-        op("P", lambda: P.transpose(out, tile("OH", t), T.ident[:]), "pT%d" % (t // 8), ["OH%d" % (t // 4), "ident"])
-    for t in range(2):
-        transpose(t)
-    mm("f3", T.f3[:, 0:1], T.U4[:, 0:128], T.Ex[:, 128:129], True, True, ["U4", "Ex"])
-    for t in range(2, NT):
-        transpose(t)
-    ts("A", T.HA[:, 16 * r:16 * r + 9], T.Ex[:, 0:129:16], T.f3[:, 0:1], None, OP.add, rd=["Ex", "Ex0", "f3", "hpad"])
-    ts("St", T.St[:, 0:129], T.Ex[:, 0:129], T.f3[:, 0:1], None, OP.add, rd=["Ex", "Ex0", "f3"])
+        def onehot_hi(t):
+            ts("OH%d" % (t // 4), tile("OH", t), T.iot8[:], T.hi[:, 16 + t:17 + t], None, OP.is_equal, rd=["hi8", "iot8"])
+        for t in range(4):
+            onehot_hi(t)
+        for l in range(8):
+            ts("OHlo", T.OHlo[:, l::8], T.hi[:, 32:48], float(l), None, OP.is_equal, rd=["lo"])
+        for t in range(4, NT):
+            onehot_hi(t)
+        for k in range(1, 4):
+            cp("U4", tile("U4", k), T.U4[:, 0:128], ["U1"])
 
-    own = tile("HA", r, 16)
-    sent = [0]
+        def transpose(t):
+            out = tile("pT%d" % (t // 8), t % 8)
+            op("P", lambda: P.transpose(out, tile("OH", t), T.ident[:]), "pT%d" % (t // 8), ["OH%d" % (t // 4), "ident"])
+        for t in range(4):
+            transpose(t)
+        for t in range(NT):
+            mm("f2", T.f2[:, t:128:16], tile("OH", t), tile("OHlo", t, 8), True, True, ["OH%d" % (t // 4), "OHlo"])
+        scan("Ex", T.Ex[:, 1:129], T.ones[:, 0:128], T.f2[:, 0:128], 0.0, ["f2", "ones"])
+        for t in range(4, 6):
+            transpose(t)
+        mm("f3", T.f3[:, 0:1], T.U4[:, 0:128], T.Ex[:, 128:129], True, True, ["U1", "Ex"])
+        for t in range(6, NT):
+            transpose(t)
+        ts("A", T.HA[:, 16 * r:16 * r + 9], T.Ex[:, 0:129:16], T.f3[:, 0:1], None, OP.add, rd=["Ex", "Ex0", "f3", "hpad"])
+        ts("St", T.St[:, 0:129], T.Ex[:, 0:129], T.f3[:, 0:1], None, OP.add, rd=["Ex", "Ex0", "f3"])
 
-    def send_counts():
-        ds = [DstId(rid=topo.addr(cores[s], core)[0], pnc=topo.addr(cores[s], core)[1]) for s in inr[r]]
-        return g.remote_dma_fused([RemoteDMATransfer(dst_ids=ds, srcs=[own], dsts=[own for s in ds], alu_op=0,
-                                                     dma_engine_mask=topo.mask(core, cores[inr[r][0]]), remote_sem=T.sem.h1)],
-                                  local_sem=T.sem.sent)
-    op("G", send_counts, "s0", ["A"], 0)
-    blk = T.HA[:, 16 * rack[0]:16 * rack[0] + 16 * len(rack)]
-    rid_c, pid_c = topo.addr(cores[cab[r]], core)
-    op("G", lambda: g.remote_dma(blk, blk, T.sem.h2, T.sem.sent, pid_c, rid_c, topo.mask(core, cores[cab[r]])), "s1", ["A", "h1"], 0)
-    sent[0] += 16
+        table = tile("HA", r, 16)
+        send("s0", ["A"], ([cores[s] for s in inr[r]], table, table, off_chip, "h1"))
+        send("sxb", ["xin"], ([other], T.xin[:, XA:TC], T.xin[:, XA:TC], stay, "xd"))
+        blk = T.HA[:, 16 * rack[0]:16 * rack[0] + 16 * len(rack)]
+        send("s1", ["A", "h1"], ([cores[c], Z[c], X[c], Z[r], other], blk, blk, off_chip, "h2"))
 
-    act("OHT0", T.OHT[:, 0:1024], T.pT0[:], ["pT0"])
-    ts("pm", T.pI[:], T.pI[:], 15, None, OP.bitwise_and, rd=["pI"])
-    tt("lin", T.lin[:], T.b16[:], T.pI[:], OP.add, ["b16", "pm"])
-    cp("rep", T.rep[:], T.pI[:, 0:8], ["pm"])
-    ts("pa", T.pa[:], T.pI[:, 0:1], float(CAPP * lp(N - 1)), None, OP.add, rd=["pm"])
-    cp("id32", T.id32[:], T.ident[:], ["ident"])
-    cp("U32", T.U32[:], T.U4[:, 0:128], ["U4"])
-    for s in range(N):
-        ms("Jc", w32(6, 9 * s, 9 * s + 9), float(CAPP * (lp(s) - lp((s - 1) % N))))
-    cp("OHT1", T.OHT[:, 1024:2048], T.pT1[:], ["pT1"])
-    mb = ["f4", "f5", "f1", "f0"]
+        cp("OHT0", T.OHT[:, 0:1024], T.pT0[:], ["pT0"])
+        act("OHT1", T.OHT[:, 1024:2048], T.pT1[:], ["pT1"])
+        mb = ["f4", "f5", "f1", "f0"]
 
-    def equal_hi(k):
-        for t in range(4 * k, 4 * k + 4):
-            mm(mb[k], tile(mb[k], t % 4), tile("OHT", t), tile("OHT", t), True, True, ["OHT%d" % (t // 8)])
-        tt("Mm%d" % k, tile("Mm", k, 512), T[mb[k]][:], T.U4[:], OP.mult, [mb[k], "U4"])
+        def equal_hi(k):
+            for t in range(4 * k, 4 * k + 4):
+                mm(mb[k], tile(mb[k], t % 4), tile("OHT", t), tile("OHT", t), True, True, ["OHT%d" % (t // 8)])
+            tt("Mm%d" % k, tile("Mm", k, 512), T[mb[k]][:], T.U4[:], OP.mult, [mb[k], "U1", "U4"])
 
-    def places(k):
-        for t in range(4 * k, 4 * k + 4):
-            o = tile("f2", t, 8)
-            mm("f2", o, tile("OHT", t), T.St[:, t:128:16], True, False, ["OHT%d" % (t // 8), "St"])
-            mm("f2", o, tile("Mm", t), tile("OHlo", t, 8), False, True, ["Mm%d" % k, "OHlo"])
-    for k in range(3):
-        equal_hi(k)
-    places(0)
-    equal_hi(3)
-    for k in range(1, 4):
-        places(k)
-    tt("prod", T.prod[:], T.f2[:, 0:128], T.OHlo[:], OP.mult, ["f2", "OHlo"])
-    scan("SC", T.SC[:], T.rm8[:], T.prod[:], 0.0, ["prod", "rm8"])
-    ts("b1", T.abf[:, 0:16], T.SC[:, 7::8], -7.5, R16, OP.add, OP.add, rd=["SC"])
-    ts("b0", T.abf[:, 16:32], T.abf[:, 0:16], -R16, None, OP.add, rd=["b1"])
-    for t in range(NT):
-        k, b = "LA%d" % (t // 2), T.abf[:, 16 + t:17 + t]
-        ts(k, tile("LA", t), T.iom[:], b, T.SC[:, 8 * t + 7:8 * t + 8], OP.add, OP.is_equal, rd=["iom", "b0", "SC"])
-        ts(k, tile("RB", t), T.iot16[:], b, T.jcol[:, t:t + 1], OP.is_equal, OP.mult, rd=["iot16", "b0", "jcol"])
-    for t in range(NT):
-        mm("f4", T.f4[:, 0:128], tile("LA", t), tile("RB", t), t == 0, t == NT - 1, ["LA%d" % (t // 2)])
+        def places(k):
+            for t in range(4 * k, 4 * k + 4):
+                o = tile("f2", t, 8)
+                mm("f2", o, tile("OHT", t), T.St[:, t:128:16], True, False, ["OHT%d" % (t // 8), "St"])
+                mm("f2", o, tile("Mm", t), tile("OHlo", t, 8), False, True, ["Mm%d" % k, "OHlo"])
+        for k in range(3):
+            equal_hi(k)
+        places(0)
+        equal_hi(3)
+        for k in range(1, 4):
+            places(k)
+        tt("prod", T.prod[:], T.f2[:, 0:128], T.OHlo[:], OP.mult, ["f2", "OHlo"])
+        scan("SC", T.SC[:], T.rm8[:], T.prod[:], 0.0, ["prod", "rm8"])
+        ts("b1", T.abf[:, 0:16], T.SC[:, 7::8], -7.5, R16, OP.add, OP.add, rd=["SC"])
+        ts("b0", T.abf[:, 16:32], T.abf[:, 0:16], -R16, None, OP.add, rd=["b1"])
+        for t in range(NT):
+            k, b = "LA%d" % t, T.abf[:, 16 + t:17 + t]
+            ts(k, tile("LA", t), iom, b, T.SC[:, 8 * t + 7:8 * t + 8], OP.add, OP.is_equal, rd=["cs", "b0", "SC"])
+            ts(k, tile("RB", t), iot16, b, T.cstf[:, 128 + t:129 + t], OP.is_equal, OP.mult, rd=["cs", "b0"])
+        for t in range(NT):
+            mm("f4", T.f4[:, 0:128], tile("LA", t), tile("RB", t), t == 0, t == NT - 1, ["LA%d" % t])
 
     def src_key(s):
-        return "A" if s == r else ("h1" if s in rack else "h2")
+        return "h2" if not own or s in far else "A" if s == r else "h1"
 
     def lengths(ss):
         for s in ss:
             tt("HT", T.HT[:, 1 + s::9], T.HA[:, 16 * s + 1:16 * s + 9], T.HA[:, 16 * s:16 * s + 8], OP.subtract, [src_key(s)])
     lengths(rack)
-    cp("invl", T.invl[:], T.f4[:, 0:128], ["f4"])
-    H = 512
-    act("xsS", T.xs[:, H:TC], T.xin[:].indirect(T.invl[:, H // 16:128]), ["xin", "invl"])
+    if own:
+        cp("invl", T.invl[:], T.f4[:, 0:128], ["f4"])
+        send("sil", ["invl"], ([other], T.invl[:], T.invl[:], on_chip, "il"))
+    h = H if own else TC // 2
+    if not third:
+        act("xsS", T.xs[:, h:TC], T.xin[:].indirect(T.invl[:, h // 16:128]), ["xin", "invl"] + ["xa"] * own)
     lengths(far)
     for i, s in enumerate(rack + far):
         mm("f5", T.f5[:, 0:8], T.ident[:], T.HA[:, 16 * s:16 * s + 8], i == 0, i == N - 1, ["ident", src_key(s)])
     cp("HT0", T.HT[:, 0::9], T.f5[:, 0:8], ["f5"])
     scan("G9", T.G9[:], T.rm9[:], T.HT[:], 0.0, ["HT", "HT0", "rm9"])
+    if third:
+        make_list(r, T, (mm, ts, tt, scan, cp), tile, w32, iot, id32, pa)
+        send("syl", ["yl"], ([other], T.yl[:], T.yl[:], off_chip, "yls"))
+        finish()
+        g.wait_ge(T.sem.sent, sent[0])
+        return
     for l in range(8):
         e = 9 * l + r
-        ts("Z", tile("Z", l, 7), T.Dd[:], T.G9[:, e:e + 1], T.HT[:, e + 1:e + 2], OP.subtract, OP.min, rd=["Dd", "G9", "HT"])
+        ts("Z", tile("Z", l, 7), Dd, T.G9[:, e:e + 1], T.HT[:, e + 1:e + 2], OP.subtract, OP.min, rd=[kc("Dd"), "G9", "HT"])
     ts("Zr", T.Zr[:], T.Z[:], 0.0, None, OP.max, rd=["Z"])
     for l in range(8):
         mm("f1", T.f1[:, 0:7], T.ones[:, 0:128], tile("Zr", l, 7), l == 0, l == 7, ["ones", "Zr"])
-    cp("xsV", T.xs[:, 0:H], T.xin[:].indirect(T.invl[:, 0:H // 16]), ["xin", "invl"])
-    peers = inr[r]
-    via = {}
-    for q in peers:
-        w, (x, k) = W[(r, cab[q])], X[(r, q)]
-        via[cab[q]] = (w, "rel0", topo.mask(core, w), 0)
-        via[q] = (x, "rel%d" % k, topo.mask(core, x) & ~topo.mask(core, cores[q]), CAPP * k)
-    via[cab[r]] = (cores[cab[r]], "dat", topo.mask(core, cores[cab[r]]), CAPP * lp(r))
-    w0, w1, w2 = [cab[q] for q in peers]
-    x0, x1, x2 = peers
-    c = cab[r]
-    for d in (w0, w1, x0, w2, x1, x2, c, r):
+    if own:
+        cp("xsV", T.xs[:, 0:h], T.xin[:].indirect(T.invl[:, 0:h // 16]), ["xin", "invl", "xa"])
+    w0, w1, w2 = [cab[q] for q in inr[r]]
+    x0, x1, x2 = inr[r]
+    for d in (w0, w1, x2, c, r) if own else (w2, x1, x0):
         if d == 0:
-            cp("off%d" % d, tile("off", d, 32), T.lin[:], ["lin"])
+            cp("off%d" % d, tile("off", d, 32), lin, [kc("lin")])
         else:
-            ts("off%d" % d, tile("off", d, 32), T.lin[:], T.f1[:, d - 1:d], None, OP.add, rd=["lin", "f1"])
+            ts("off%d" % d, tile("off", d, 32), lin, T.f1[:, d - 1:d], None, OP.add, rd=[kc("lin"), "f1"])
+    if not own:
+        cp("xsV", T.xs[:, 0:h], T.xin[:].indirect(T.invl[:, 0:h // 16]), ["xin", "invl"])
 
     def gather(f, d, a=0, b=CAPP):
         o = CAPP * lp(r) if d == r else CAPP * d
         f("st%d_%d" % (d, a), T["land" if d == r else "stage"][:, o + a:o + b], T.xs[:].indirect(T.off[:, 32 * d + a // 16:32 * d + b // 16]),
           ["xsS", "xsV", "xpad", "off%d" % d])
 
-    def half(m, i):
-        e = [b for b in range(m.bit_length()) if m >> b & 1]
-        return sum(1 << b for b in e[i * len(e) // 2:(i + 1) * len(e) // 2])
+    def block(d, a, b, m, sem):
+        to = W[(r, d)] if (r, d) in W else cores[d]
+        o = 0 if (r, d) in W else CAPP * lp(r)
+        return ([to], T.stage[:, CAPP * d + a:CAPP * d + b], T.land[:, o + a:o + b], m, sem)
+    M = CAPP // 2
 
-    def ship(*blocks):
-        trs = []
-        for d, a, b, sem, m in blocks:
-            to, s0, m0, o = via[d]
-            rid, pid = topo.addr(to, core)
-            trs.append(RemoteDMATransfer(dst_ids=[DstId(rid=rid, pnc=pid)], srcs=[T.stage[:, CAPP * d + a:CAPP * d + b]],
-                                         dsts=[T.land[:, o + a:o + b]], alu_op=0, dma_engine_mask=m or m0, remote_sem=T.sem[sem or s0]))
-            sent[0] += bin(m or m0).count("1")
-        op("G", lambda: g.remote_dma_fused(trs, local_sem=T.sem.sent), "s_%d_%d" % blocks[0][:2], ["st%d_%d" % b[:2] for b in blocks], 0)
+    def rest(d, m, *cuts):
+        send("sr%d" % d, ["st%d_%d" % (d, a) for a in (C0,) + cuts], block(d, C0, CAPP, m, "rel"))
 
-    def rest(d):
-        return (d, C0, CAPP, None, None)
-    early = (w1, x0, w2, x1)
-    gather(act, w0)
-    for d in early:
-        gather(act, d, 0, C0)
-    for f, d in ((cp, w1), (act, x0), (cp, w2), (act, x1)):
-        gather(f, d, C0)
-    for d in (x2, c, r):
+    def whole(d):
         gather(act, d)
-    ship((w0, 0, CAPP, None, None))
-    ship(*[(d, 0, C0, "relw", half(via[d][2], i // 2)) for i, d in enumerate(early)])
-    ship(rest(w1), rest(x0))
-    ship(rest(w2), rest(x1))
-    ship((x2, 0, CAPP, None, None), (c, 0, CAPP, None, None))
+        send("sx%d" % d, ["st%d_0" % d], block(d, 0, CAPP, off_chip, "dat"))
+    early = ((w0, act, half(off_chip, 0)), (w1, cp, half(off_chip, 1)), (x2, cp, half(stay, 0))) if own else (
+        (w2, act, half(off_chip, 0)), (x1, cp, half(stay, 0)))
+    for d, f, m in early:
+        gather(f, d, 0, C0)
+    send("sw", ["st%d_0" % d for d, f, m in early], *[block(d, 0, C0, m, "relw") for d, f, m in early])
+    if own:
+        gather(act, w0, C0)
+        rest(w0, off_chip)
+        gather(cp, w1, C0)
+        rest(w1, off_chip)
+        whole(c)
+        gather(cp, x2, C0)
+        rest(x2, stay)
+        gather(act, r)
+    else:
+        gather(cp, w2, M)
+        gather(act, w2, C0, M)
+        rest(w2, off_chip, M)
+        gather(cp, x1, C0)
+        rest(x1, stay)
+        whole(x0)
+        finish()
+        g.wait_ge(T.sem.sent, sent[0])
+        return
 
+    for k in range(4):
+        (cp if k % 2 == 0 else act)("y%d" % k, T.yout[:, YC[k]:YC[k + 1]], T.land[:].indirect(T.yl[:, YC[k] // 16:YC[k + 1] // 16]),
+                                    ["yl", "dat", "st%d_0" % r])
+    for k in range(4):
+        dma("yo", T.y[:, YC[k]:YC[k + 1]], T.yout[:, YC[k]:YC[k + 1]], ["y%d" % k])
+    op("Y", lambda: None, "end", ["yo"], 0)
+    finish()
+    g.wait_ge(T.sem.sent, sent[0])
+
+
+def make_list(r, T, calls, tile, w32, iot, id32, pa):
+    mm, ts, tt, scan, cp = calls
     ts("q1", w32(0), T.G9[:], -1.0, float(TC * r), OP.mult, OP.add, rd=["G9"])
     ts("gp", T.gp[:, 144:216], T.G9[:], float(TC * r), 0.0, OP.subtract, OP.max, rd=["G9"])
     tt("q2", w32(1, 0, 71), w32(0, 0, 71), T.HT[:, 1:72], OP.min, ["q1", "HT", "HT0"])
@@ -363,42 +443,33 @@ def rank_program(g, core, T, topo):
     for a in range(16):
         ts("LS", T.LS[:, a::16], T.ga[:], float(a), None, OP.is_equal, rd=["ga"])
     for s in range(N):
-        ts("a1", w32(2, 9 * s, 9 * s + 9), T.HA[:, 16 * s:16 * s + 9], T.f3[:, s:s + 1], 0.0, OP.subtract, OP.max, rd=["f3", "h1", "h2", "A"])
+        ts("a1", w32(2, 9 * s, 9 * s + 9), T.HA[:, 16 * s:16 * s + 9], T.f3[:, s:s + 1], 0.0, OP.subtract, OP.max, rd=["f3", "h2"])
     ts("a2", w32(3), w32(2), float(CAPP), None, OP.min, rd=["a1"])
     tt("dl", w32(4, 9, 72), w32(3, 9, 72), w32(3, 1, 64), OP.subtract, ["a2"])
     tt("dl", w32(4, 0, 8), w32(3, 0, 8), w32(3, 63, 71), OP.subtract, ["a2"])
-    ms("dl", w32(4, 8, 9), 0.0)
-    tt("dl2", w32(5), w32(4), w32(6), OP.add, ["dl", "Jc"])
+    tt("dl2", w32(5), w32(4), w32(6), OP.add, ["dl", "dlz", "Jc"])
     for i in range(64):
         l, s = i // N, i % N
         e = 9 * l + s
-        ts("sg%d" % (i // 4), tile("RS", i), T.iot[:], T.gb[:, e:e + 1], w32(5, 9 * s + l, 9 * s + l + 1), OP.is_equal, OP.mult,
-           rd=["iot", "gb", "dl2"])
+        ts("sg%d" % (i // 4), tile("RS", i), iot, T.gb[:, e:e + 1], w32(5, 9 * s + l, 9 * s + l + 1), OP.is_equal, OP.mult,
+           rd=["cst", "gb", "dl2"])
     for i in range(64):
         mm("f4", T.f4[:, 0:16], tile("RS", i), tile("LS", 9 * (i // N) + i % N, 16), i == 0, i == 63, ["sg%d" % (i // 4), "LS"])
     scan("E", T.E[:], T.ones[:, 0:16], T.f4[:, 0:16], 0.0, ["f4", "ones"])
     ts("Rr", T.Rr[:], T.ones[:, 0:128], T.E[:, 15:16], 16.0, OP.mult, OP.add, rd=["E", "ones"])
     mm("f2", T.f2[:, 0:128], T.Rr[:], T.U32[:], True, False, ["Rr", "U32"])
     cp("Er", T.Er[:], T.E[:].indirect(T.rep[:]), ["E", "rep"])
-    mm("f2", T.f2[:, 0:128], T.Er[:], T.id32[:], False, True, ["Er", "id32"])
-    ts("yl", T.yl[:], T.f2[:, 0:128], T.pa[:], None, OP.add, rd=["f2", "pa"])
-    for k in range(4):
-        (cp if k % 2 == 0 else act)("y%d" % k, T.yout[:, YC[k]:YC[k + 1]], T.land[:].indirect(T.yl[:, YC[k] // 16:YC[k + 1] // 16]),
-                                    ["yl", "dat", "st%d_0" % r])
-    for k in range(4):
-        dma("yo", T.y[:, YC[k]:YC[k + 1]], T.yout[:, YC[k]:YC[k + 1]], ["y%d" % k])
-    op("Y", lambda: None, "end", ["yo"], 0)
-    finish()
-    g.wait_ge(T.sem.sent, sent[0])
+    mm("f2", T.f2[:, 0:128], T.Er[:], id32, False, True, ["Er", "id32"])
+    ts("yl", T.yl[:], T.f2[:, 0:128], pa, None, OP.add, rd=["f2", "pa"])
 
 
 def helper(g, core, T, topo, jobs, cores):
-    for s, d, k, a, b in jobs:
+    for s, d, a, b in jobs:
         rid, pid = topo.addr(cores[d], core)
         if b < CAPP:
             g.wait_ge(T.sem.relw, 4)
         else:
-            g.wait_ge(T.sem["rel%d" % k], 8)
-        o, i = CAPP * lp(s), CAPP * k
-        g.remote_dma(T.land[:, o + a:o + b], T.land[:, i + a:i + b], T.sem.dat, T.sem.sent, pid, rid, topo.mask(core, cores[d]))
+            g.wait_ge(T.sem.rel, 8)
+        o = CAPP * lp(s)
+        g.remote_dma(T.land[:, o + a:o + b], T.land[:, a:b], T.sem.dat, T.sem.sent, pid, rid, topo.mask(core, cores[d]))
     g.wait_ge(T.sem.sent, 8 * len(jobs))

@@ -3,11 +3,16 @@ from concourse.mybir import AluOpType as OP, ActivationFunctionType as AF
 
 N, TC, CAPP, NT = 8, 2048, 512, 16
 CORES_ALL = 512
-C0 = 64
-XA = 128
-H = 512
+K = 4
+NL = NT // K
+BLK = CAPP + 16
+PARTS = ((0, 256), (256, BLK))
+M = 288
+XA, XB = 128, 1152
+SW = 48
 R8, R16 = 1.5 * 2 ** 26, 1.5 * 2 ** 27
 YC = (0, 512, 1024, 1536, 2048)
+IOM = ([[0, 8], [1, 16]], 0, 0)
 SCRATCH = {}
 
 
@@ -19,18 +24,18 @@ def _buf(dtype, rows, **cols):
 _buf("int32", 16, kI=128)
 _buf("bfloat16", 16, zsel=240)
 _buf("float16", 16, kF=128)
-_buf("int32", 128, pI=32, gp=216)
-_buf("uint16", 128, invl=128, off=256, yl=128, rep=8)
-_buf("float16", 128, HA=128, Ex=144, St=144, RB=2048, Zr=56, q3=72, LS=1152, RS=8192)
-_buf("bfloat16", 128, ones=512, iot8=128, cst=384, ident=128, U4=512, OH=2048, OHlo=128, OHT=2048, Mm=2048,
-     rm8=128, rm9=72, LA=2048, xin=2048, xs=2560, stage=4096, land=4096, yout=2048, ga=72)
-_buf("float32", 128, cstf=192, hi=48, b16=32, prod=128, SC=128, abf=32, HT=72, G9=72, Z=56, w32=504, gb=72,
-     U32=128, E=16, Er=128, Rr=128)
-for _k in range(2):
-    SCRATCH["pT%d" % _k] = ("psum", [128, 1024], "bfloat16")
+_buf("int32", 128, pI=16, gp=216)
+_buf("uint16", 128, off=3 * SW, sh=12, yl=128)
+_buf("float16", 128, HA=128, At=16, Ex=144, St=144, RB=128 * NL, q3=72, RS=4096, PL=128 * K)
+_buf("bfloat16", 128, ones=128, iot=240, iot8=128, iot16=128, iom=128, ident=128, U4=512, OH=2048, OHlo=128, OHT=128 * NL,
+     Mm=128 * NL, rm8=56, rm9=72, LA=128 * NL, xin=2048, stage=3 * BLK, land=N * BLK, yout=2048, LS=1152)
+_buf("float32", 128, hi=48, pc=2, lin0=8, cst=32, ylp=256, be0=8, be=8, prod=8 * NL, SC=8 * NL, Jd=2 * NL,
+     HT=72, G9=72, invF=128 + SW, w32=432, gb=72, U32=128, id32=128, pa=2, E=16, Er=128, Rr=128)
+SCRATCH["pT0"] = ("psum", [128, 1024], "bfloat16")
 for _k in range(6):
     SCRATCH["f%d" % _k] = ("psum", [128, 512], "float32")
-SEMAPHORES = ["h1", "h2", "dat", "cs", "xd", "il", "yls", "relw", "rel", "sent"] + ["e%d" % _k for _k in range(138)]
+SEMAPHORES = ["h1", "h2", "h3", "ca", "cb", "cc", "ci", "dat", "hs", "ss", "pl", "xd0", "xd1", "xd2", "yls", "rel0", "rel1", "sent"]
+SEMAPHORES += ["e%d" % _k for _k in range(120)]
 
 
 def lp(r):
@@ -47,23 +52,23 @@ def plan(T, topo):
     inr = {r: sorted([s for s in racks[r] if s != r], key=lambda s: (s - r) % len(racks[r])) for r in range(N)}
     cab = {r: [s for s in range(N) if s not in racks[r] and topo.may_write(cores[r], cores[s])
                and topo.chip(cores[s]) == topo.chip(cores[r])][0] for r in range(N)}
-    W, X, Z, role, mine = {}, {}, {}, {}, {}
+    W, X, Z, role, mine, gives = {}, {}, {}, {}, {}, {}
     for q in range(N):
         L = chip_of(cores[q], topo)
         wl = [L[i] for i in range(0, len(L), 2) if cores[q] not in L[i:i + 2]]
-        pairs = [(w, s, cab[q]) for s, w in zip(inr[q], wl)]
-        X[q] = [x for x in L if topo.die(x) != topo.die(cores[q]) and x not in wl][0]
-        spare = [x for x in L if x not in wl and x not in (cores[q], X[q])]
-        for x, d in ((X[q], inr[q][1]), (cores[q], inr[q][2])):
-            w = [w for w in spare if topo.die(w) == topo.die(x)][0]
-            pairs.append((w, q, d))
-            spare.remove(w)
-        Z[q] = spare[0]
-        mine[X[q]] = mine[Z[q]] = q
-        for w, s, d in pairs:
-            W[(s, d)] = w
-            role[w] = [(s, d, a, b) for a, b in ((0, C0), (C0, CAPP))]
-    return cores, racks, inr, cab, W, X, Z, role, mine
+        for s, w in zip(inr[q], wl):
+            W[(s, cab[q])] = w
+            role[w] = (s, cab[q])
+        spare = [x for x in L if x not in wl and x != cores[q]]
+        there = [x for x in spare if topo.die(x) != topo.die(cores[q])]
+        here = [x for x in spare if x not in there]
+        X[q] = [cores[q]] + there[:2] + here[:1]
+        Z[q] = [here[1]] + [w for w in wl if topo.die(w) == topo.die(cores[q])][:1]
+        for w, x in zip([w for w in wl if w not in Z[q]], (X[q][1], X[q][3])):
+            gives[w] = x
+        for x in X[q][1:] + Z[q]:
+            mine[x] = q
+    return cores, racks, inr, cab, W, X, Z, role, mine, gives
 
 
 def program(g, T):
@@ -132,34 +137,62 @@ def half(m, i):
 
 
 def rank_program(g, core, T, topo):
-    cores, racks, inr, cab, W, X, Z, role, mine = plan(T, topo)
+    cores, racks, inr, cab, W, X, Z, role, mine, gives = plan(T, topo)
     own = T.rank_of(core) is not None
     if not own and core not in mine:
         if core in role:
-            helper(g, core, T, topo, role[core], cores)
+            n, relay = helper(g, core, T, topo, role[core], cores)
+            g.iota(T.iom[:], *IOM, allow_small_or_imprecise_dtypes=True).then_inc(T.sem.e0, 1)
+            g.wait_ge(T.sem.e0, 1)
+            rid, pid = topo.addr(gives[core], core)
+            g.remote_dma(T.iom[:], T.iom[:], T.sem.cb, T.sem.sent, pid, rid, topo.mask(core, cores[role[core][1]]))
+            for q in range(len(PARTS)):
+                g.wait_ge(T.sem["rel%d" % q], n)
+                relay(q)
+            g.wait_ge(T.sem.sent, n * (len(PARTS) + 1))
         return
     r = T.rank_of(core) if own else mine[core]
-    third = core == Z[r]
+    lister = core in Z[r]
+    k = -1 if lister else X[r].index(core)
+    zi = Z[r].index(core) if lister else -1
     V, S, P, Y = g.vector, g.scalar, g.tensor, g.sync
     op, external, finish = program(g, T)
     rack = racks[r]
     far = [s for s in range(N) if s not in rack]
-    c, other = cab[r], X[r] if own else cores[r]
+    c, team = cab[r], X[r]
     off_chip = topo.mask(core, cores[inr[r][0]])
-    on_chip = topo.mask(core, other)
+    on_chip = topo.mask(core, team[1] if own else cores[r])
     stay = on_chip & ~off_chip
+    n_off, n_on, n_stay = count_bits(off_chip), count_bits(on_chip), count_bits(stay)
     sent = [0]
-    if own:
-        external("h1", "h1", 8 * (len(rack) - 1))
-        external("h2", "h2", 8)
-        external("cs", "cs", 2 * 8)
-        external("yl", "yls", 8)
-        external("dat", "dat", 8 * (N - 1) + 8 * sum((s, r) in W for s in range(N)))
+    external("h2", "h2", n_off)
+    if zi == 0:
+        external("h3", "h1", n_off * (len(rack) - 1) + n_stay)
     else:
-        external("h2", "h2", 2 * 8)
-        if not third:
-            external("xin", "xd", count_bits(on_chip) + count_bits(stay))
-            external("invl", "il", count_bits(on_chip))
+        external("h3", "h3", n_stay)
+    if own:
+        external("ylp", "yls", n_on * len(Z[r]))
+        external("ca", "ca", n_on)
+        external("cb", "cb", n_on)
+        external("cc", "cc", n_on)
+        external("dat", "dat", n_off * sum(len(PARTS) if (s, r) in W else 1 for s in range(N) if s != r))
+        xr = ["xa", "xb"]
+    elif not lister:
+        if k in (1, 3):
+            external("xa", "xd0", n_on // 2)
+            external("xb", "xd1", n_on // 2)
+            external("xc", "xd2", 2 * n_on)
+            external("iom", "cb", n_off)
+            xr = ["xa", "xb", "xc"]
+        else:
+            external("xc", "xd2", 4 * n_on)
+            xr = ["xc"]
+        external("hi8", "hs", n_on)
+        external("St", "ss", n_on)
+    elif zi == 0:
+        external("iot", "ci", n_on)
+    if not lister:
+        external("PLx", "pl", (K - 1) * n_on)
 
     def mm(key, out, lhs, rhs, a, b, rd):
         op("P", lambda: P.matmul(out, lhs, rhs, a, b), key, rd)
@@ -191,9 +224,6 @@ def rank_program(g, core, T, topo):
     def iota(key, ap, pat, base, cm):
         op("G", lambda: g.iota(ap, pat, base, cm, allow_small_or_imprecise_dtypes=True), key)
 
-    def aff(key, ap, in_, pat, cmp, base, cm, rd):
-        op("G", lambda: g.affine_select(ap, in_, pat, cmp, 0.0, base, cm), key, rd)
-
     def send(name, rd, *trs):
         def call():
             L = []
@@ -205,62 +235,123 @@ def rank_program(g, core, T, topo):
         sent[0] += sum(count_bits(tr[3]) for tr in trs)
         op("G", call, name, rd, 0)
 
+    def onehot(key, out, apart_key, apart, in_, m, n, pieces, rd):
+        for v in range(m):
+            op("S", lambda v=v: S.activation(apart[:, v:n:m], in_, AF.Abs, bias=-float(v)), apart_key, rd)
+        for i in range(pieces):
+            a, b = n * i // pieces, n * (i + 1) // pieces
+            op("S", lambda a=a, b=b: S.activation(out[:, a:b], apart[:, a:b], AF.Relu, bias=1.0, scale=-1.0), "%s%d" % (key, i), [apart_key])
+
     def w32(i, a=0, b=72):
         return T.w32[:, 72 * i + a:72 * i + b]
 
     def tile(buf, t, n=128):
         return T[buf][:, n * t:n * t + n]
 
-    iom, iot16, iot = [tile("cst", i) for i in range(3)]
-    id32, jcol, lin, Dd, pa, pm8 = [T.cstf[:, i:j] for i, j in ((0, 128), (128, 144), (144, 176), (176, 183), (183, 184), (184, 192))]
+    def lin(n):
+        return T.cst[:, 0:n]
+
+    def Dd(n):
+        return T.cst[:, 8:8 + n]
+
+    def jcol(t, n=1):
+        return T.cst[:, 16 + t:16 + t + n]
+
     if own:
         dma("kI", T.kI[:], T.key[:])
-        dma("xa", T.xin[:, 0:XA], T.x[:, 0:XA])
-        dma("xin", T.xin[:, XA:TC], T.x[:, XA:TC])
+        dma("xa", T.xin[:, 0:2 * XA], T.x[:, 0:2 * XA])
+        dma("xb", T.xin[:, 2 * XA:TC], T.x[:, 2 * XA:TC])
+    iota("pc", T.pc[:], [[0, 2]], 0, 1)
+    if zi != 0:
+        iota("iot", T.iot[:], [[1, 240]], 0, 0)
+    if own:
+        send("sci", ["iot"], ([Z[r][0]], T.iot[:], T.iot[:], on_chip, "ci"))
+    p0 = T.pc[:, 0:1]
     ms("ones", T.ones[:], 1.0)
     ms("rm9a", T.rm9[:], 1.0)
-    if not third:
-        ms("xpad", T.xs[:, TC:TC + CAPP], 0.0)
-    if own:
-        aff("zsel", T.zsel[:], T.ones[0:16, 0:240], [[1, 240]], OP.is_equal, -112, -1, ["ones"])
-        iota("iot8", T.iot8[:], [[8, 128]], 0, 0)
-        aff("ident", T.ident[:], T.ones[:, 0:128], [[1, 128]], OP.is_equal, 0, -1, ["ones"])
-        aff("U1", T.U4[:, 0:128], T.ones[:, 0:128], [[1, 128]], OP.is_gt, 0, -1, ["ones"])
-        send("sxa", ["xa"], ([other], T.xin[:, 0:XA], T.xin[:, 0:XA], on_chip, "xd"))
+    if not lister:
         ms("rm8a", T.rm8[:], 1.0)
-        ms("hpad", tile("HA", r, 16), 0.0)
-        ms("Ex0", T.Ex[:, 0:1], 0.0)
+        ms("invP", T.invF[:, 128:128 + SW], 0.0)
+        ms("be_0", T.be[:, 0:1], 0.0)
         ms("rm8", T.rm8[:, 0::8], 0.0, ["rm8a"])
-        ms("rm9", T.rm9[:, 0::9], 0.0, ["rm9a"])
-    else:
-        if third:
-            iota("cst", iom, [[0, 8], [1, 16]], 0, 0)
-            iota("cst", iot16, [[16, 128]], 0, 0)
-            iota("cst", iot, [[1, 128]], 0, 0)
-            send("scs", ["cst"], ([other], T.cst[:], T.cst[:], off_chip, "cs"))
-        iota("pI", T.pI[:], [[0, 32]], 0, 1)
-        iota("b16", T.b16[:], [[16, 32]], 0, 0)
-        aff("ident", T.ident[:], T.ones[:, 0:128], [[1, 128]], OP.is_equal, 0, -1, ["ones"])
+    ms("rm9", T.rm9[:, 0::9], 0.0, ["rm9a"])
+    if zi == 1:
+        iota("iom", T.iom[:], *IOM)
+        send("scb", ["iom"], ([cores[r]], T.iom[:], T.iom[:], on_chip, "cb"))
+    if not own:
+        iota("pI", T.pI[:], [[0, 16]], 0, 1)
+        iota("lin0", T.lin0[:], [[16, 8]], 0, 0)
+        iota("Dd", Dd(8), [[TC, 8]], TC, 0)
+        iota("jcol", jcol(0, 16), [[128, 16]], 0, 1)
+    if zi == 0:
         ts("pm", T.pI[:], T.pI[:], 15, None, OP.bitwise_and, rd=["pI"])
-        cp("pm8", pm8, T.pI[:, 0:8], ["pm"])
-        ts("pa", pa, T.pI[:, 0:1], float(CAPP * lp(N - 1)), None, OP.add, rd=["pm"])
-        cp("id32", id32, T.ident[:], ["ident"])
-        ms("rm9", T.rm9[:, 0::9], 0.0, ["rm9a"])
-        if third:
-            aff("U1", T.U4[:, 0:128], T.ones[:, 0:128], [[1, 128]], OP.is_gt, 0, -1, ["ones"])
-            for s in range(N):
-                ms("Jc", w32(6, 9 * s, 9 * s + 9), float(CAPP * (lp(s) - lp((s - 1) % N))))
-            ms("dlz", w32(4, 8, 9), 0.0)
-            cp("rep", T.rep[:], T.pI[:, 0:8], ["pm"])
-            cp("U32", T.U32[:], T.U4[:, 0:128], ["U1"])
-        else:
-            iota("jcol", jcol, [[128, 16]], 0, 1)
-            iota("Dd", Dd, [[TC, 7]], TC, 0)
-            tt("lin", lin, T.b16[:], T.pI[:], OP.add, ["b16", "pm"])
-            send("scs", ["jcol", "Dd", "lin", "pm8", "pa", "id32"], ([other], T.cstf[:], T.cstf[:], off_chip, "cs"))
+        tt("lin", lin(8), T.lin0[:], T.pI[:, 0:8], OP.add, ["lin0", "pm"])
+        send("sca", ["lin", "Dd", "jcol"], ([cores[r]], T.cst[:], T.cst[:], on_chip, "ca"))
+    if own:
+        ms("hpad", T.At[:], 0.0)
+        ms("Ex0", T.Ex[:, 0:1], 0.0)
+        ts("zsel", T.zsel[:], T.iot[0:16, :], -112.0, T.pc[0:16, 0:1], OP.add, OP.is_equal, rd=["iot", "pc"])
+    if k == 2:
+        ts("iot16", T.iot16[:], T.iot[:, 0:128], 16.0, None, OP.mult, rd=["iot"])
+        send("scc", ["iot16"], ([cores[r]], T.iot16[:], T.iot16[:], on_chip, "cc"))
+        iota("iom", T.iom[:], *IOM)
+    if not lister:
+        ts("iot8", T.iot8[:], T.iot[:, 0:128], 8.0, None, OP.mult, rd=["iot"])
+    ts("ident", T.ident[:], T.iot[:, 0:128], p0, None, OP.is_equal, rd=["iot", "pc"])
+    for i in range(1 if lister else 4):
+        ts("U4", tile("U4", i), T.iot[:, 0:128], p0, None, OP.is_gt, rd=["iot", "pc"])
+    if k in (1, 3):
+        ts("iot16", T.iot16[:], T.iot[:, 0:128], 16.0, None, OP.mult, rd=["iot"])
+    if not own and zi != 0:
+        ts("pm", T.pI[:], T.pI[:], 15, None, OP.bitwise_and, rd=["pI"])
+        tt("lin", lin(8), T.lin0[:], T.pI[:, 0:8], OP.add, ["lin0", "pm"])
+    if lister:
+        cp("id32", T.id32[:], T.ident[:], ["ident"])
+        cp("U32", T.U32[:], T.U4[:, 0:128], ["U4"])
+        cp("rep", T.sh[:, 0:8], T.pI[:, 0:8], ["pm"])
+        ts("pa", T.pa[:], T.pI[:, 0:2], float(BLK * lp(N - 1)), None, OP.add, rd=["pm"])
 
-    def kc(k):
-        return "cs" if own else k
+    def kc(name):
+        return name if not own else {"iom": "cb", "iot16": "cc"}.get(name, "ca")
+
+    def places_of_runs():
+        def src_key(s):
+            return "h2" if s in far else "h3"
+        for s in rack + far:
+            tt("HT", T.HT[:, 1 + s::9], T.HA[:, 16 * s + 1:16 * s + 9], T.HA[:, 16 * s:16 * s + 8], OP.subtract, [src_key(s)])
+        for i, s in enumerate(rack + far):
+            mm("f5", T.f5[:, 0:8], T.ident[:], T.HA[:, 16 * s:16 * s + 8], i == 0, i == N - 1, ["ident", src_key(s)])
+        cp("HT0", T.HT[:, 0::9], T.f5[:, 0:8], ["f5"])
+        scan("G9", T.G9[:], T.rm9[:], T.HT[:], 0.0, ["HT", "HT0", "rm9"])
+
+    if lister:
+        if zi == 0:
+            blk = T.HA[:, 16 * rack[0]:16 * rack[0] + 16 * len(rack)]
+            send("s1", ["h3"], (X[c][1:] + Z[c] + X[c][:1], blk, blk, off_chip, "h2"), (team[1:] + Z[r][1:] + team[:1], blk, blk, stay, "h3"))
+        places_of_runs()
+        make_list(r, zi, T, (mm, ts, tt, scan, cp, onehot), tile, w32)
+        if core in role:
+            n, relay = helper(g, core, T, topo, role[core], cores)
+            for q in range(len(PARTS)):
+                external("rel%d" % q, "rel%d" % q, n)
+                op("G", lambda q=q: relay(q), "sr%d" % q, ["rel%d" % q], 0)
+            sent[0] += n * len(PARTS)
+        part = tile("ylp", zi)
+        send("syl", ["ylp"], ([cores[r]], part, part, on_chip, "yls"))
+        finish()
+        g.wait_ge(T.sem.sent, sent[0])
+        return
+
+    def pass_on(a, b):
+        piece = T.xin[:, a:b]
+        return ([team[3 if k == 1 else 1], team[2]], piece, piece, on_chip, "xd2")
+    if own:
+        send("sxa", ["xa"], ([team[1]], T.xin[:, 0:XA], T.xin[:, 0:XA], half(on_chip, 0), "xd0"),
+             ([team[3]], T.xin[:, XA:2 * XA], T.xin[:, XA:2 * XA], half(on_chip, 1), "xd0"))
+    elif k == 1:
+        send("fxa", ["xa"], pass_on(0, XA))
+    elif k == 3:
+        send("fxa", ["xa"], pass_on(XA, 2 * XA))
 
     if own:
         cp("kF", T.kF[:], T.kI[:], ["kI"])
@@ -269,207 +360,188 @@ def rank_program(g, core, T, topo):
         ts("hi1", T.hi[:, 0:16], T.f0[:, 0:16], -3.5, R8, OP.add, OP.add, rd=["f0"])
         ts("hi8", T.hi[:, 16:32], T.hi[:, 0:16], -R8, None, OP.add, rd=["hi1"])
         tt("lo", T.hi[:, 32:48], T.f0[:, 0:16], T.hi[:, 16:32], OP.subtract, ["f0", "hi8"])
-
-        def onehot_hi(t):
+        send("shi", ["hi8", "lo"], (team[1:], T.hi[:, 16:48], T.hi[:, 16:48], on_chip, "hs"))
+        onehot("OHlo", T.OHlo, "Mm", T.Mm, T.hi[:, 32:48], 8, 128, 1, ["lo"])
+        for t in range(NT):
             ts("OH%d" % (t // 4), tile("OH", t), T.iot8[:], T.hi[:, 16 + t:17 + t], None, OP.is_equal, rd=["hi8", "iot8"])
-        for t in range(4):
-            onehot_hi(t)
+        for t in range(NT):
+            mm("f2", T.f2[:, t:128:16], tile("OH", t), tile("OHlo", t, 8), True, True, ["OH%d" % (t // 4), "OHlo0"])
+    else:
+        for i in range(NL):
+            t = 16 + NL * k + i
+            ts("OH0", tile("OH", i), T.iot8[:], T.hi[:, t:t + 1], None, OP.is_equal, rd=["hi8", "iot8"])
         for l in range(8):
-            ts("OHlo", T.OHlo[:, l::8], T.hi[:, 32:48], float(l), None, OP.is_equal, rd=["lo"])
-        for t in range(4, NT):
-            onehot_hi(t)
-        for k in range(1, 4):
-            cp("U4", tile("U4", k), T.U4[:, 0:128], ["U1"])
+            t = 32 + NL * k
+            ts("OHlo0", T.OHlo[:, l:8 * NL:8], T.hi[:, t:t + NL], float(l), None, OP.is_equal, rd=["hi8"])
 
-        def transpose(t):
-            out = tile("pT%d" % (t // 8), t % 8)
-            op("P", lambda: P.transpose(out, tile("OH", t), T.ident[:]), "pT%d" % (t // 8), ["OH%d" % (t // 4), "ident"])
-        for t in range(4):
-            transpose(t)
-        for t in range(NT):
-            mm("f2", T.f2[:, t:128:16], tile("OH", t), tile("OHlo", t, 8), True, True, ["OH%d" % (t // 4), "OHlo"])
-        scan("Ex", T.Ex[:, 1:129], T.ones[:, 0:128], T.f2[:, 0:128], 0.0, ["f2", "ones"])
-        for t in range(4, 6):
-            transpose(t)
-        mm("f3", T.f3[:, 0:1], T.U4[:, 0:128], T.Ex[:, 128:129], True, True, ["U1", "Ex"])
-        for t in range(6, NT):
-            transpose(t)
-        ts("A", T.HA[:, 16 * r:16 * r + 9], T.Ex[:, 0:129:16], T.f3[:, 0:1], None, OP.add, rd=["Ex", "Ex0", "f3", "hpad"])
-        ts("St", T.St[:, 0:129], T.Ex[:, 0:129], T.f3[:, 0:1], None, OP.add, rd=["Ex", "Ex0", "f3"])
-
-        table = tile("HA", r, 16)
-        send("s0", ["A"], ([cores[s] for s in inr[r]], table, table, off_chip, "h1"))
-        send("sxb", ["xin"], ([other], T.xin[:, XA:TC], T.xin[:, XA:TC], stay, "xd"))
-        blk = T.HA[:, 16 * rack[0]:16 * rack[0] + 16 * len(rack)]
-        send("s1", ["A", "h1"], ([cores[c], Z[c], X[c], Z[r], other], blk, blk, off_chip, "h2"))
-
-        cp("OHT0", T.OHT[:, 0:1024], T.pT0[:], ["pT0"])
-        act("OHT1", T.OHT[:, 1024:2048], T.pT1[:], ["pT1"])
-        mb = ["f4", "f5", "f1", "f0"]
-
-        def equal_hi(k):
-            for t in range(4 * k, 4 * k + 4):
-                mm(mb[k], tile(mb[k], t % 4), tile("OHT", t), tile("OHT", t), True, True, ["OHT%d" % (t // 8)])
-            tt("Mm%d" % k, tile("Mm", k, 512), T[mb[k]][:], T.U4[:], OP.mult, [mb[k], "U1", "U4"])
-
-        def places(k):
-            for t in range(4 * k, 4 * k + 4):
-                o = tile("f2", t, 8)
-                mm("f2", o, tile("OHT", t), T.St[:, t:128:16], True, False, ["OHT%d" % (t // 8), "St"])
-                mm("f2", o, tile("Mm", t), tile("OHlo", t, 8), False, True, ["Mm%d" % k, "OHlo"])
-        for k in range(3):
-            equal_hi(k)
-        places(0)
-        equal_hi(3)
-        for k in range(1, 4):
-            places(k)
-        tt("prod", T.prod[:], T.f2[:, 0:128], T.OHlo[:], OP.mult, ["f2", "OHlo"])
-        scan("SC", T.SC[:], T.rm8[:], T.prod[:], 0.0, ["prod", "rm8"])
-        ts("b1", T.abf[:, 0:16], T.SC[:, 7::8], -7.5, R16, OP.add, OP.add, rd=["SC"])
-        ts("b0", T.abf[:, 16:32], T.abf[:, 0:16], -R16, None, OP.add, rd=["b1"])
-        for t in range(NT):
-            k, b = "LA%d" % t, T.abf[:, 16 + t:17 + t]
-            ts(k, tile("LA", t), iom, b, T.SC[:, 8 * t + 7:8 * t + 8], OP.add, OP.is_equal, rd=["cs", "b0", "SC"])
-            ts(k, tile("RB", t), iot16, b, T.cstf[:, 128 + t:129 + t], OP.is_equal, OP.mult, rd=["cs", "b0"])
-        for t in range(NT):
-            mm("f4", T.f4[:, 0:128], tile("LA", t), tile("RB", t), t == 0, t == NT - 1, ["LA%d" % t])
-
-    def src_key(s):
-        return "h2" if not own or s in far else "A" if s == r else "h1"
-
-    def lengths(ss):
-        for s in ss:
-            tt("HT", T.HT[:, 1 + s::9], T.HA[:, 16 * s + 1:16 * s + 9], T.HA[:, 16 * s:16 * s + 8], OP.subtract, [src_key(s)])
-    lengths(rack)
+    def transpose(i):
+        out = tile("pT0", i)
+        op("P", lambda: P.transpose(out, tile("OH", i), T.ident[:]), "pT0", ["OH0", "ident"])
     if own:
-        cp("invl", T.invl[:], T.f4[:, 0:128], ["f4"])
-        send("sil", ["invl"], ([other], T.invl[:], T.invl[:], on_chip, "il"))
-    h = H if own else TC // 2
-    if not third:
-        act("xsS", T.xs[:, h:TC], T.xin[:].indirect(T.invl[:, h // 16:128]), ["xin", "invl"] + ["xa"] * own)
-    lengths(far)
-    for i, s in enumerate(rack + far):
-        mm("f5", T.f5[:, 0:8], T.ident[:], T.HA[:, 16 * s:16 * s + 8], i == 0, i == N - 1, ["ident", src_key(s)])
-    cp("HT0", T.HT[:, 0::9], T.f5[:, 0:8], ["f5"])
-    scan("G9", T.G9[:], T.rm9[:], T.HT[:], 0.0, ["HT", "HT0", "rm9"])
-    if third:
-        make_list(r, T, (mm, ts, tt, scan, cp), tile, w32, iot, id32, pa)
-        send("syl", ["yl"], ([other], T.yl[:], T.yl[:], off_chip, "yls"))
-        finish()
-        g.wait_ge(T.sem.sent, sent[0])
-        return
+        scan("Ex", T.Ex[:, 1:129], T.ones[:], T.f2[:, 0:128], 0.0, ["f2", "ones"])
+        for i in range(2):
+            transpose(i)
+        mm("f3", T.f3[:, 0:1], T.U4[:, 0:128], T.Ex[:, 128:129], True, True, ["U4", "Ex"])
+        for i in range(2, NL):
+            transpose(i)
+        ts("A", T.At[:, 0:9], T.Ex[:, 0:129:16], T.f3[:, 0:1], None, OP.add, rd=["Ex", "Ex0", "f3", "hpad"])
+        ts("St", T.St[:, 0:129], T.Ex[:, 0:129], T.f3[:, 0:1], None, OP.add, rd=["Ex", "Ex0", "f3"])
+        table = tile("HA", r, 16)
+        send("s0", ["A"], ([Z[x][0] for x in inr[r]], T.At[:], table, off_chip, "h1"), ([Z[r][0]], T.At[:], table, stay, "h1"))
+        send("sst", ["St"], (team[1:], T.St[:, 0:128], T.St[:, 0:128], on_chip, "ss"))
+        send("sxb", ["xb"], ([team[1]], T.xin[:, 2 * XA:XB], T.xin[:, 2 * XA:XB], half(on_chip, 0), "xd1"),
+             ([team[3]], T.xin[:, XB:TC], T.xin[:, XB:TC], half(on_chip, 1), "xd1"))
+    else:
+        for i in range(NL):
+            transpose(i)
+
+    cp("OHT", T.OHT[:], T.pT0[:, 0:128 * NL], ["pT0"])
+    for i in range(NL):
+        mm("f4", tile("f4", i), tile("OHT", i), tile("OHT", i), True, True, ["OHT"])
+    tt("Mm", T.Mm[:], T.f4[:, 0:128 * NL], T.U4[:, 0:128 * NL], OP.mult, ["f4", "U4"])
+    for i in range(NL):
+        o = tile("f2", i, 8)
+        mm("f2", o, tile("OHT", i), T.St[:, NL * k + i:128:16], True, False, ["OHT", "St"])
+        mm("f2", o, tile("Mm", i), tile("OHlo", i, 8), False, True, ["Mm", "OHlo0"])
+    tt("prod", T.prod[:], T.f2[:, 0:8 * NL], T.OHlo[:, 0:8 * NL], OP.mult, ["f2", "OHlo0"])
+    scan("SC", T.SC[:], T.rm8[:, 0:8 * NL], T.prod[:], 0.0, ["prod", "rm8"])
+    ts("b1", T.Jd[:, 0:NL], T.SC[:, 7::8], -7.5, R16, OP.add, OP.add, rd=["SC"])
+    ts("b0", T.Jd[:, NL:2 * NL], T.Jd[:, 0:NL], -R16, None, OP.add, rd=["b1"])
+    for i in range(NL):
+        key, b, t = "LA%d" % i, T.Jd[:, NL + i:NL + i + 1], NL * k + i
+        ts(key, tile("LA", i), T.iom[:], b, T.SC[:, 8 * i + 7:8 * i + 8], OP.add, OP.is_equal, rd=[kc("iom"), "b0", "SC"])
+        ts(key, tile("RB", i), T.iot16[:], b, jcol(t), OP.is_equal, OP.mult, rd=[kc("iot16"), kc("jcol"), "b0"])
+    for i in range(NL):
+        mm("f0", T.f0[:, 0:128], tile("LA", i), tile("RB", i), i == 0, i == NL - 1, ["LA%d" % i])
+    mine_pl = tile("PL", k)
+    cp("PL", mine_pl, T.f0[:, 0:128], ["f0"])
+    send("spl", ["PL"], ([x for x in team if x != core], mine_pl, mine_pl, on_chip, "pl"))
+    if k in (1, 3):
+        send("fxb", ["xb"], pass_on(2 * XA, XB) if k == 1 else pass_on(XB, TC))
+
+    places_of_runs()
     for l in range(8):
         e = 9 * l + r
-        ts("Z", tile("Z", l, 7), Dd, T.G9[:, e:e + 1], T.HT[:, e + 1:e + 2], OP.subtract, OP.min, rd=[kc("Dd"), "G9", "HT"])
-    ts("Zr", T.Zr[:], T.Z[:], 0.0, None, OP.max, rd=["Z"])
-    for l in range(8):
-        mm("f1", T.f1[:, 0:7], T.ones[:, 0:128], tile("Zr", l, 7), l == 0, l == 7, ["ones", "Zr"])
-    if own:
-        cp("xsV", T.xs[:, 0:h], T.xin[:].indirect(T.invl[:, 0:h // 16]), ["xin", "invl", "xa"])
-    w0, w1, w2 = [cab[q] for q in inr[r]]
+        ts("Z", T.w32[:, l:56:8], Dd(7), T.G9[:, e:e + 1], T.HT[:, e + 1:e + 2], OP.subtract, OP.min, rd=[kc("Dd"), "G9", "HT"])
+    ts("Zr", T.q3[:, 0:56], T.w32[:, 0:56], 0.0, None, OP.max, rd=["Z"])
+    mm("f1", T.f1[:, 0:56], T.ones[:], T.q3[:, 0:56], True, True, ["ones", "Zr"])
+    scan("SB", T.gb[:, 0:56], T.rm8[:], T.f1[:, 0:56], 0.0, ["f1", "rm8"])
+    ts("be0", T.be0[:, 0:7], T.gb[:, 7:56:8], -7.5, R16, OP.add, OP.add, rd=["SB"])
+    ts("be", T.be[:, 1:8], T.be0[:, 0:7], -R16, 0.0625, OP.add, OP.mult, rd=["be0"])
     x0, x1, x2 = inr[r]
-    for d in (w0, w1, x2, c, r) if own else (w2, x1, x0):
-        if d == 0:
-            cp("off%d" % d, tile("off", d, 32), lin, [kc("lin")])
-        else:
-            ts("off%d" % d, tile("off", d, 32), lin, T.f1[:, d - 1:d], None, OP.add, rd=[kc("lin"), "f1"])
-    if not own:
-        cp("xsV", T.xs[:, 0:h], T.xin[:].indirect(T.invl[:, 0:h // 16]), ["xin", "invl"])
+    w0, w1, w2 = [cab[q] for q in inr[r]]
+    blocks = ((c, x2, r), (w0, x0), (w1,), (w2, x1))[k]
+    for i, d in enumerate(blocks):
+        ts("sh%d" % i, T.sh[:, 4 * i:4 * i + 3], lin(3), T.be[:, d:d + 1], None, OP.add, rd=[kc("lin"), "be", "be_0"])
+    for i in range(K):
+        mm("f3", T.f3[:, 0:128], T.ident[:], tile("PL", i), i == 0, i == K - 1, ["ident", "PL" if i == k else "PLx"])
+    cp("invF", T.invF[:, 0:128], T.f3[:, 0:128], ["f3"])
 
-    def gather(f, d, a=0, b=CAPP):
-        o = CAPP * lp(r) if d == r else CAPP * d
-        f("st%d_%d" % (d, a), T["land" if d == r else "stage"][:, o + a:o + b], T.xs[:].indirect(T.off[:, 32 * d + a // 16:32 * d + b // 16]),
-          ["xsS", "xsV", "xpad", "off%d" % d])
+    def cut(i):
+        cp("off%d" % i, T.off[:, SW * i:SW * i + SW], T.invF[:].indirect(T.sh[:, 4 * i:4 * i + 3]), ["invF", "invP", "sh%d" % i])
 
-    def block(d, a, b, m, sem):
+    def gather(f, i, a, b):
+        o = BLK * (lp(r) if blocks[i] == r else i)
+        f("st%d_%d" % (i, a), T["land" if blocks[i] == r else "stage"][:, o + a:o + b],
+          T.xin[:].indirect(T.off[:, SW * i + a // 16:SW * i + b // 16]), xr + ["off%d" % i])
+
+    def ship(i, a, b, keys, sem):
+        d = blocks[i]
         to = W[(r, d)] if (r, d) in W else cores[d]
-        o = 0 if (r, d) in W else CAPP * lp(r)
-        return ([to], T.stage[:, CAPP * d + a:CAPP * d + b], T.land[:, o + a:o + b], m, sem)
-    M = CAPP // 2
-
-    def rest(d, m, *cuts):
-        send("sr%d" % d, ["st%d_%d" % (d, a) for a in (C0,) + cuts], block(d, C0, CAPP, m, "rel"))
-
-    def whole(d):
-        gather(act, d)
-        send("sx%d" % d, ["st%d_0" % d], block(d, 0, CAPP, off_chip, "dat"))
-    early = ((w0, act, half(off_chip, 0)), (w1, cp, half(off_chip, 1)), (x2, cp, half(stay, 0))) if own else (
-        (w2, act, half(off_chip, 0)), (x1, cp, half(stay, 0)))
-    for d, f, m in early:
-        gather(f, d, 0, C0)
-    send("sw", ["st%d_0" % d for d, f, m in early], *[block(d, 0, C0, m, "relw") for d, f, m in early])
-    if own:
-        gather(act, w0, C0)
-        rest(w0, off_chip)
-        gather(cp, w1, C0)
-        rest(w1, off_chip)
-        whole(c)
-        gather(cp, x2, C0)
-        rest(x2, stay)
-        gather(act, r)
-    else:
-        gather(cp, w2, M)
-        gather(act, w2, C0, M)
-        rest(w2, off_chip, M)
-        gather(cp, x1, C0)
-        rest(x1, stay)
-        whole(x0)
+        o = 0 if (r, d) in W else BLK * lp(r)
+        send("sb%d_%d" % (i, a), ["st%d_%d" % (i, z) for z in keys],
+             ([to], T.stage[:, BLK * i + a:BLK * i + b], T.land[:, o + a:o + b], off_chip, sem))
+    for i, d in enumerate(blocks):
+        cut(i)
+        if (r, d) in W:
+            for f, (a, b) in zip((act, cp), PARTS):
+                gather(f, i, a, b)
+            for q, (a, b) in enumerate(PARTS):
+                ship(i, a, b, [a], "rel%d" % q)
+        else:
+            gather(cp, i, 0, M)
+            gather(act, i, M, BLK)
+            if d != r:
+                ship(i, 0, BLK, [0, M], "dat")
+    if not own:
         finish()
         g.wait_ge(T.sem.sent, sent[0])
         return
 
-    for k in range(4):
-        (cp if k % 2 == 0 else act)("y%d" % k, T.yout[:, YC[k]:YC[k + 1]], T.land[:].indirect(T.yl[:, YC[k] // 16:YC[k + 1] // 16]),
-                                    ["yl", "dat", "st%d_0" % r])
-    for k in range(4):
-        dma("yo", T.y[:, YC[k]:YC[k + 1]], T.yout[:, YC[k]:YC[k + 1]], ["y%d" % k])
+    tt("yl32", T.Rr[:], T.ylp[:, 0:128], T.ylp[:, 128:256], OP.add, ["ylp"])
+    cp("yl", T.yl[:], T.Rr[:], ["yl32"])
+    for q in range(4):
+        (cp if q % 2 == 0 else act)("y%d" % q, T.yout[:, YC[q]:YC[q + 1]], T.land[:].indirect(T.yl[:, YC[q] // 16:YC[q + 1] // 16]),
+                                    ["yl", "dat", "st2_0", "st2_%d" % M])
+    for q in range(4):
+        dma("yo", T.y[:, YC[q]:YC[q + 1]], T.yout[:, YC[q]:YC[q + 1]], ["y%d" % q])
     op("Y", lambda: None, "end", ["yo"], 0)
     finish()
     g.wait_ge(T.sem.sent, sent[0])
 
 
-def make_list(r, T, calls, tile, w32, iot, id32, pa):
-    mm, ts, tt, scan, cp = calls
+def make_list(r, zi, T, calls, tile, w32):
+    mm, ts, tt, scan, cp, onehot = calls
+    ss = list(range(N // 2 * zi, N // 2 * zi + N // 2))
+    al, pb, ga = T.SC[:, 0:8], T.prod[:, 0:1], T.LA[:, 0:72]
     ts("q1", w32(0), T.G9[:], -1.0, float(TC * r), OP.mult, OP.add, rd=["G9"])
     ts("gp", T.gp[:, 144:216], T.G9[:], float(TC * r), 0.0, OP.subtract, OP.max, rd=["G9"])
     tt("q2", w32(1, 0, 71), w32(0, 0, 71), T.HT[:, 1:72], OP.min, ["q1", "HT", "HT0"])
-    ts("gab32", T.gp[:, 72:144], T.gp[:, 144:216], 4, None, OP.arith_shift_right, rd=["gp"])
     ts("gab32", T.gp[:, 0:72], T.gp[:, 144:216], 15, None, OP.bitwise_and, rd=["gp"])
+    ts("gab32", T.gp[:, 72:144], T.gp[:, 144:216], 4, None, OP.arith_shift_right, rd=["gp"])
     ts("q3", T.q3[:, 0:71], w32(1, 0, 71), 0.0, None, OP.max, rd=["q2"])
     for l in range(8):
-        mm("f3", T.f3[:, 0:8], T.ones[:, 0:128], T.q3[:, 9 * l:9 * l + 8], l == 0, l == 7, ["ones", "q3"])
-    cp("ga", T.ga[:], T.gp[:, 0:72], ["gab32"])
+        mm("f3", T.f3[:, 0:8], T.ones[:], T.q3[:, 9 * l:9 * l + 8], l == 0, l == 7, ["ones", "q3"])
+    cp("ga", ga, T.gp[:, 0:72], ["gab32"])
     cp("gb", T.gb[:], T.gp[:, 72:144], ["gab32"])
-    for a in range(16):
-        ts("LS", T.LS[:, a::16], T.ga[:], float(a), None, OP.is_equal, rd=["ga"])
-    for s in range(N):
-        ts("a1", w32(2, 9 * s, 9 * s + 9), T.HA[:, 16 * s:16 * s + 9], T.f3[:, s:s + 1], 0.0, OP.subtract, OP.max, rd=["f3", "h2"])
-    ts("a2", w32(3), w32(2), float(CAPP), None, OP.min, rd=["a1"])
-    tt("dl", w32(4, 9, 72), w32(3, 9, 72), w32(3, 1, 64), OP.subtract, ["a2"])
-    tt("dl", w32(4, 0, 8), w32(3, 0, 8), w32(3, 63, 71), OP.subtract, ["a2"])
-    tt("dl2", w32(5), w32(4), w32(6), OP.add, ["dl", "dlz", "Jc"])
-    for i in range(64):
-        l, s = i // N, i % N
+    onehot("LS", T.LS, "apart", T.stage, ga, 16, 1152, 4, ["ga"])
+    ts("be0", T.be0[:], T.f3[:, 0:8], -7.5, R16, OP.add, OP.add, rd=["f3"])
+    for s in [(ss[0] - 1) % N] + ss:
+        ts("a1", w32(2, 9 * s, 9 * s + 9), T.HA[:, 16 * s:16 * s + 9], T.f3[:, s:s + 1], 0.0, OP.subtract, OP.max,
+           rd=["f3", "h2", "h3"])
+    ts("be", T.be[:], T.be0[:], -R16, None, OP.add, rd=["be0"])
+    lo, hi = 9 * ss[0], 9 * ss[-1] + 9
+    for a, b in ((lo - 9, hi),) if zi else ((lo, hi), (63, 72)):
+        ts("a2", w32(3, a, b), w32(2, a, b), float(CAPP), None, OP.min, rd=["a1"])
+    tt("al", al, T.f3[:, 0:8], T.be[:], OP.subtract, ["f3", "be"])
+    if zi:
+        tt("dl", w32(4, lo, hi), w32(3, lo, hi), w32(3, lo - 8, hi - 8), OP.subtract, ["a2"])
+    else:
+        tt("dl", w32(4, 9, hi), w32(3, 9, hi), w32(3, 1, hi - 8), OP.subtract, ["a2"])
+        tt("dl", w32(4, 0, 8), w32(3, 0, 8), w32(3, 63, 71), OP.subtract, ["a2"])
+    tt("Jd", T.Jd[:, 1:8], T.SC[:, 1:8], T.SC[:, 0:7], OP.subtract, ["al"])
+    tt("Jd", T.Jd[:, 0:1], T.SC[:, 0:1], T.SC[:, 7:8], OP.subtract, ["al"])
+    if zi:
+        ts("pb", pb, T.pa[:, 0:1], T.SC[:, 7:8], None, OP.add, rd=["pa", "al"])
+    for s in ss:
+        ts("dl2", w32(5, 9 * s, 9 * s + 8), w32(4, 9 * s, 9 * s + 8), T.Jd[:, s:s + 1], float(BLK * (lp(s) - lp((s - 1) % N))),
+           OP.add, OP.add, rd=["dl", "Jd"])
+    runs = [(l, s) for l in range(8) for s in ss]
+    n = len(runs)
+    for i, (l, s) in enumerate(runs):
         e = 9 * l + s
-        ts("sg%d" % (i // 4), tile("RS", i), iot, T.gb[:, e:e + 1], w32(5, 9 * s + l, 9 * s + l + 1), OP.is_equal, OP.mult,
-           rd=["cst", "gb", "dl2"])
-    for i in range(64):
-        mm("f4", T.f4[:, 0:16], tile("RS", i), tile("LS", 9 * (i // N) + i % N, 16), i == 0, i == 63, ["sg%d" % (i // 4), "LS"])
+        ts("sg%d" % (i // 4), tile("RS", i), T.iot[:, 0:128], T.gb[:, e:e + 1], w32(5, 9 * s + l, 9 * s + l + 1), OP.is_equal, OP.mult,
+           rd=["iot", "gb", "dl2"])
+    for i, (l, s) in enumerate(runs):
+        mm("f4", T.f4[:, 0:16], tile("RS", i), tile("LS", 9 * l + s, 16), i == 0, i == n - 1, ["sg%d" % (i // 4), "LS%d" % (l // 2)])
     scan("E", T.E[:], T.ones[:, 0:16], T.f4[:, 0:16], 0.0, ["f4", "ones"])
-    ts("Rr", T.Rr[:], T.ones[:, 0:128], T.E[:, 15:16], 16.0, OP.mult, OP.add, rd=["E", "ones"])
+    ts("Rr", T.Rr[:], T.ones[:], T.E[:, 15:16], 16.0 * zi, OP.mult, OP.add, rd=["E", "ones"])
     mm("f2", T.f2[:, 0:128], T.Rr[:], T.U32[:], True, False, ["Rr", "U32"])
-    cp("Er", T.Er[:], T.E[:].indirect(T.rep[:]), ["E", "rep"])
-    mm("f2", T.f2[:, 0:128], T.Er[:], id32, False, True, ["Er", "id32"])
-    ts("yl", T.yl[:], T.f2[:, 0:128], pa, None, OP.add, rd=["f2", "pa"])
+    cp("Er", T.Er[:], T.E[:].indirect(T.sh[:, 0:8]), ["E", "rep"])
+    mm("f2", T.f2[:, 0:128], T.Er[:], T.id32[:], False, True, ["Er", "id32"])
+    if zi:
+        ts("ylp", tile("ylp", zi), T.f2[:, 0:128], pb, None, OP.add, rd=["f2", "pb"])
+    else:
+        cp("ylp", tile("ylp", zi), T.f2[:, 0:128], ["f2"])
 
 
-def helper(g, core, T, topo, jobs, cores):
-    for s, d, a, b in jobs:
-        rid, pid = topo.addr(cores[d], core)
-        if b < CAPP:
-            g.wait_ge(T.sem.relw, 4)
-        else:
-            g.wait_ge(T.sem.rel, 8)
-        o = CAPP * lp(s)
-        g.remote_dma(T.land[:, o + a:o + b], T.land[:, a:b], T.sem.dat, T.sem.sent, pid, rid, topo.mask(core, cores[d]))
-    g.wait_ge(T.sem.sent, 8 * len(jobs))
+def helper(g, core, T, topo, job, cores):
+    s, d = job
+    rid, pid = topo.addr(cores[d], core)
+    m = topo.mask(core, cores[d])
+
+    def relay(q):
+        a, b = PARTS[q]
+        o = BLK * lp(s)
+        return g.remote_dma(T.land[:, o + a:o + b], T.land[:, a:b], T.sem.dat, T.sem.sent, pid, rid, m)
+    return count_bits(m), relay

from concourse.bass import DstId, RemoteDMATransfer
from concourse.mybir import AluOpType as OP, ActivationFunctionType as AF

N, TC, CAPP, NT = 8, 2048, 512, 16
CORES_ALL = 512
K = 4
NL = NT // K
BLK = CAPP + 16
PARTS = ((0, 256), (256, BLK))
M = 288
XA, XB = 128, 1152
SW = 48
R8, R16 = 1.5 * 2 ** 26, 1.5 * 2 ** 27
YC = (0, 512, 1024, 1536, 2048)
IOM = ([[0, 8], [1, 16]], 0, 0)
SCRATCH = {}


def _buf(dtype, rows, **cols):
    for k, n in cols.items():
        SCRATCH[k] = ("sbuf", [rows, n], dtype)


_buf("int32", 16, kI=128)
_buf("bfloat16", 16, zsel=240)
_buf("float16", 16, kF=128)
_buf("int32", 128, pI=16, gp=216)
_buf("uint16", 128, off=3 * SW, sh=12, yl=128)
_buf("float16", 128, HA=128, At=16, Ex=144, St=144, RB=128 * NL, q3=72, RS=4096, PL=128 * K)
_buf("bfloat16", 128, ones=128, iot=240, iot8=128, iot16=128, iom=128, ident=128, U4=512, OH=2048, OHlo=128, OHT=128 * NL,
     Mm=128 * NL, rm8=56, rm9=72, LA=128 * NL, xin=2048, stage=3 * BLK, land=N * BLK, yout=2048, LS=1152)
_buf("float32", 128, hi=48, pc=2, lin0=8, cst=32, ylp=256, be0=8, be=8, prod=8 * NL, SC=8 * NL, Jd=2 * NL,
     HT=72, G9=72, invF=128 + SW, w32=432, gb=72, U32=128, id32=128, pa=2, E=16, Er=128, Rr=128)
SCRATCH["pT0"] = ("psum", [128, 1024], "bfloat16")
for _k in range(6):
    SCRATCH["f%d" % _k] = ("psum", [128, 512], "float32")
SEMAPHORES = ["h1", "h2", "h3", "ca", "cb", "cc", "ci", "dat", "hs", "ss", "pl", "xd0", "xd1", "xd2", "yls", "rel0", "rel1", "sent"]
SEMAPHORES += ["e%d" % _k for _k in range(120)]


def lp(r):
    return 2 * r if r < N // 2 else 2 * N - 1 - 2 * r


def chip_of(c, topo):
    return [x for x in range(CORES_ALL) if topo.host(x) == topo.host(c) and topo.chip(x) == topo.chip(c)]


def plan(T, topo):
    cores = [int(c) for c in T.cores]
    racks = {r: [s for s in range(N) if topo.rack(topo.host(cores[s])) == topo.rack(topo.host(cores[r]))] for r in range(N)}
    inr = {r: sorted([s for s in racks[r] if s != r], key=lambda s: (s - r) % len(racks[r])) for r in range(N)}
    cab = {r: [s for s in range(N) if s not in racks[r] and topo.may_write(cores[r], cores[s])
               and topo.chip(cores[s]) == topo.chip(cores[r])][0] for r in range(N)}
    W, X, Z, role, mine, gives = {}, {}, {}, {}, {}, {}
    for q in range(N):
        L = chip_of(cores[q], topo)
        wl = [L[i] for i in range(0, len(L), 2) if cores[q] not in L[i:i + 2]]
        for s, w in zip(inr[q], wl):
            W[(s, cab[q])] = w
            role[w] = (s, cab[q])
        spare = [x for x in L if x not in wl and x != cores[q]]
        there = [x for x in spare if topo.die(x) != topo.die(cores[q])]
        here = [x for x in spare if x not in there]
        X[q] = [cores[q]] + there[:2] + here[:1]
        Z[q] = [here[1]] + [w for w in wl if topo.die(w) == topo.die(cores[q])][:1]
        for w, x in zip([w for w in wl if w not in Z[q]], (X[q][1], X[q][3])):
            gives[w] = x
        for x in X[q][1:] + Z[q]:
            mine[x] = q
    return cores, racks, inr, cab, W, X, Z, role, mine, gives


def program(g, T):
    Q = {"G": g, "V": g.vector, "S": g.scalar, "P": g.tensor, "Y": g.sync}
    ops, cur, known, order = [], {}, {q: set() for q in Q}, []

    def gen(q, ext=None, total=0):
        x = {"n": len(order), "q": q, "open": True, "readers": [], "waited": ext is not None, "sem": ext, "total": total, "known": set()}
        order.append(x)
        return x

    def external(key, sem, total):
        cur[key] = gen(None, sem, total)
        cur[key]["open"] = False

    def op(q, fn, w, r=(), inc=1):
        need = [cur[k] for k in r]
        old = cur.get(w)
        if old is not None and old["open"] and old["q"] == q and w not in r:
            me = old
        else:
            if old is not None:
                need += [old] + old["readers"]
            me = gen(q)
        waits = []
        for x in sorted(need, key=lambda z: -z["n"]):
            if x is me:
                continue
            x["open"] = False
            if x["n"] not in known[q]:
                x["waited"] = True
                waits.append(x)
                known[q].add(x["n"])
                known[q] |= x["known"]
        for k in r:
            if me not in cur[k]["readers"]:
                cur[k]["readers"].append(me)
        cur[w] = me
        me["total"] += inc
        me["known"] |= known[q]
        ops.append((q, fn, me, waits, inc))

    def finish():
        free = 0
        for x in order:
            if x["waited"] and x["sem"] is None:
                x["sem"] = "e%d" % free
                free += 1
        for q, fn, me, waits, inc in ops:
            for x in waits:
                Q[q].wait_ge(T.sem[x["sem"]], x["total"])
            ins = fn()
            if me["waited"] and inc:
                ins.then_inc(T.sem[me["sem"]], inc)

    return op, external, finish


def count_bits(m):
    return bin(m).count("1")


def half(m, i):
    e = [b for b in range(m.bit_length()) if m >> b & 1]
    return sum(1 << b for b in e[i * len(e) // 2:(i + 1) * len(e) // 2])


def rank_program(g, core, T, topo):
    cores, racks, inr, cab, W, X, Z, role, mine, gives = plan(T, topo)
    own = T.rank_of(core) is not None
    if not own and core not in mine:
        if core in role:
            n, relay = helper(g, core, T, topo, role[core], cores)
            g.iota(T.iom[:], *IOM, allow_small_or_imprecise_dtypes=True).then_inc(T.sem.e0, 1)
            g.wait_ge(T.sem.e0, 1)
            rid, pid = topo.addr(gives[core], core)
            g.remote_dma(T.iom[:], T.iom[:], T.sem.cb, T.sem.sent, pid, rid, topo.mask(core, cores[role[core][1]]))
            for q in range(len(PARTS)):
                g.wait_ge(T.sem["rel%d" % q], n)
                relay(q)
            g.wait_ge(T.sem.sent, n * (len(PARTS) + 1))
        return
    r = T.rank_of(core) if own else mine[core]
    lister = core in Z[r]
    k = -1 if lister else X[r].index(core)
    zi = Z[r].index(core) if lister else -1
    V, S, P, Y = g.vector, g.scalar, g.tensor, g.sync
    op, external, finish = program(g, T)
    rack = racks[r]
    far = [s for s in range(N) if s not in rack]
    c, team = cab[r], X[r]
    off_chip = topo.mask(core, cores[inr[r][0]])
    on_chip = topo.mask(core, team[1] if own else cores[r])
    stay = on_chip & ~off_chip
    n_off, n_on, n_stay = count_bits(off_chip), count_bits(on_chip), count_bits(stay)
    sent = [0]
    external("h2", "h2", n_off)
    if zi == 0:
        external("h3", "h1", n_off * (len(rack) - 1) + n_stay)
    else:
        external("h3", "h3", n_stay)
    if own:
        external("ylp", "yls", n_on * len(Z[r]))
        external("ca", "ca", n_on)
        external("cb", "cb", n_on)
        external("cc", "cc", n_on)
        external("dat", "dat", n_off * sum(len(PARTS) if (s, r) in W else 1 for s in range(N) if s != r))
        xr = ["xa", "xb"]
    elif not lister:
        if k in (1, 3):
            external("xa", "xd0", n_on // 2)
            external("xb", "xd1", n_on // 2)
            external("xc", "xd2", 2 * n_on)
            external("iom", "cb", n_off)
            xr = ["xa", "xb", "xc"]
        else:
            external("xc", "xd2", 4 * n_on)
            xr = ["xc"]
        external("hi8", "hs", n_on)
        external("St", "ss", n_on)
    elif zi == 0:
        external("iot", "ci", n_on)
    if not lister:
        external("PLx", "pl", (K - 1) * n_on)

    def mm(key, out, lhs, rhs, a, b, rd):
        op("P", lambda: P.matmul(out, lhs, rhs, a, b), key, rd)

    def ts(key, out, in0, s1, s2, o0, o1=None, rd=()):
        if o1 is None:
            op("V", lambda: V.tensor_scalar(out, in0, s1, None, o0), key, rd)
        else:
            op("V", lambda: V.tensor_scalar(out, in0, s1, s2, o0, o1), key, rd)

    def tt(key, out, in0, in1, o, rd=()):
        op("V", lambda: V.tensor_tensor(out, in0, in1, o), key, rd)

    def scan(key, out, d0, d1, init, rd):
        op("V", lambda: V.tensor_tensor_scan(out, d0, d1, init, OP.mult, OP.add), key, rd)

    def cp(key, out, in_, rd=()):
        op("V", lambda: V.tensor_copy(out, in_), key, rd)

    def act(key, out, in_, rd=()):
        op("S", lambda: S.activation(out, in_, AF.Copy), key, rd)

    def ms(key, ap, v, rd=()):
        op("V", lambda: V.memset(ap, v), key, rd)

    def dma(key, out, in_, rd=()):
        op("Y", lambda: Y.dma_start(out, in_), key, rd, 16)

    def iota(key, ap, pat, base, cm):
        op("G", lambda: g.iota(ap, pat, base, cm, allow_small_or_imprecise_dtypes=True), key)

    def send(name, rd, *trs):
        def call():
            L = []
            for to, src, dst, m, sem in trs:
                ad = [topo.addr(t, core) for t in to]
                L.append(RemoteDMATransfer(dst_ids=[DstId(rid=i, pnc=p) for i, p in ad], srcs=[src], dsts=[dst for t in to], alu_op=0,
                                           dma_engine_mask=m, remote_sem=T.sem[sem]))
            return g.remote_dma_fused(L, local_sem=T.sem.sent)
        sent[0] += sum(count_bits(tr[3]) for tr in trs)
        op("G", call, name, rd, 0)

    def onehot(key, out, apart_key, apart, in_, m, n, pieces, rd):
        for v in range(m):
            op("S", lambda v=v: S.activation(apart[:, v:n:m], in_, AF.Abs, bias=-float(v)), apart_key, rd)
        for i in range(pieces):
            a, b = n * i // pieces, n * (i + 1) // pieces
            op("S", lambda a=a, b=b: S.activation(out[:, a:b], apart[:, a:b], AF.Relu, bias=1.0, scale=-1.0), "%s%d" % (key, i), [apart_key])

    def w32(i, a=0, b=72):
        return T.w32[:, 72 * i + a:72 * i + b]

    def tile(buf, t, n=128):
        return T[buf][:, n * t:n * t + n]

    def lin(n):
        return T.cst[:, 0:n]

    def Dd(n):
        return T.cst[:, 8:8 + n]

    def jcol(t, n=1):
        return T.cst[:, 16 + t:16 + t + n]

    if own:
        dma("kI", T.kI[:], T.key[:])
        dma("xa", T.xin[:, 0:2 * XA], T.x[:, 0:2 * XA])
        dma("xb", T.xin[:, 2 * XA:TC], T.x[:, 2 * XA:TC])
    iota("pc", T.pc[:], [[0, 2]], 0, 1)
    if zi != 0:
        iota("iot", T.iot[:], [[1, 240]], 0, 0)
    if own:
        send("sci", ["iot"], ([Z[r][0]], T.iot[:], T.iot[:], on_chip, "ci"))
    p0 = T.pc[:, 0:1]
    ms("ones", T.ones[:], 1.0)
    ms("rm9a", T.rm9[:], 1.0)
    if not lister:
        ms("rm8a", T.rm8[:], 1.0)
        ms("invP", T.invF[:, 128:128 + SW], 0.0)
        ms("be_0", T.be[:, 0:1], 0.0)
        ms("rm8", T.rm8[:, 0::8], 0.0, ["rm8a"])
    ms("rm9", T.rm9[:, 0::9], 0.0, ["rm9a"])
    if zi == 1:
        iota("iom", T.iom[:], *IOM)
        send("scb", ["iom"], ([cores[r]], T.iom[:], T.iom[:], on_chip, "cb"))
    if not own:
        iota("pI", T.pI[:], [[0, 16]], 0, 1)
        iota("lin0", T.lin0[:], [[16, 8]], 0, 0)
        iota("Dd", Dd(8), [[TC, 8]], TC, 0)
        iota("jcol", jcol(0, 16), [[128, 16]], 0, 1)
    if zi == 0:
        ts("pm", T.pI[:], T.pI[:], 15, None, OP.bitwise_and, rd=["pI"])
        tt("lin", lin(8), T.lin0[:], T.pI[:, 0:8], OP.add, ["lin0", "pm"])
        send("sca", ["lin", "Dd", "jcol"], ([cores[r]], T.cst[:], T.cst[:], on_chip, "ca"))
    if own:
        ms("hpad", T.At[:], 0.0)
        ms("Ex0", T.Ex[:, 0:1], 0.0)
        ts("zsel", T.zsel[:], T.iot[0:16, :], -112.0, T.pc[0:16, 0:1], OP.add, OP.is_equal, rd=["iot", "pc"])
    if k == 2:
        ts("iot16", T.iot16[:], T.iot[:, 0:128], 16.0, None, OP.mult, rd=["iot"])
        send("scc", ["iot16"], ([cores[r]], T.iot16[:], T.iot16[:], on_chip, "cc"))
        iota("iom", T.iom[:], *IOM)
    if not lister:
        ts("iot8", T.iot8[:], T.iot[:, 0:128], 8.0, None, OP.mult, rd=["iot"])
    ts("ident", T.ident[:], T.iot[:, 0:128], p0, None, OP.is_equal, rd=["iot", "pc"])
    for i in range(1 if lister else 4):
        ts("U4", tile("U4", i), T.iot[:, 0:128], p0, None, OP.is_gt, rd=["iot", "pc"])
    if k in (1, 3):
        ts("iot16", T.iot16[:], T.iot[:, 0:128], 16.0, None, OP.mult, rd=["iot"])
    if not own and zi != 0:
        ts("pm", T.pI[:], T.pI[:], 15, None, OP.bitwise_and, rd=["pI"])
        tt("lin", lin(8), T.lin0[:], T.pI[:, 0:8], OP.add, ["lin0", "pm"])
    if lister:
        cp("id32", T.id32[:], T.ident[:], ["ident"])
        cp("U32", T.U32[:], T.U4[:, 0:128], ["U4"])
        cp("rep", T.sh[:, 0:8], T.pI[:, 0:8], ["pm"])
        ts("pa", T.pa[:], T.pI[:, 0:2], float(BLK * lp(N - 1)), None, OP.add, rd=["pm"])

    def kc(name):
        return name if not own else {"iom": "cb", "iot16": "cc"}.get(name, "ca")

    def places_of_runs():
        def src_key(s):
            return "h2" if s in far else "h3"
        for s in rack + far:
            tt("HT", T.HT[:, 1 + s::9], T.HA[:, 16 * s + 1:16 * s + 9], T.HA[:, 16 * s:16 * s + 8], OP.subtract, [src_key(s)])
        for i, s in enumerate(rack + far):
            mm("f5", T.f5[:, 0:8], T.ident[:], T.HA[:, 16 * s:16 * s + 8], i == 0, i == N - 1, ["ident", src_key(s)])
        cp("HT0", T.HT[:, 0::9], T.f5[:, 0:8], ["f5"])
        scan("G9", T.G9[:], T.rm9[:], T.HT[:], 0.0, ["HT", "HT0", "rm9"])

    if lister:
        if zi == 0:
            blk = T.HA[:, 16 * rack[0]:16 * rack[0] + 16 * len(rack)]
            send("s1", ["h3"], (X[c][1:] + Z[c] + X[c][:1], blk, blk, off_chip, "h2"), (team[1:] + Z[r][1:] + team[:1], blk, blk, stay, "h3"))
        places_of_runs()
        make_list(r, zi, T, (mm, ts, tt, scan, cp, onehot), tile, w32)
        if core in role:
            n, relay = helper(g, core, T, topo, role[core], cores)
            for q in range(len(PARTS)):
                external("rel%d" % q, "rel%d" % q, n)
                op("G", lambda q=q: relay(q), "sr%d" % q, ["rel%d" % q], 0)
            sent[0] += n * len(PARTS)
        part = tile("ylp", zi)
        send("syl", ["ylp"], ([cores[r]], part, part, on_chip, "yls"))
        finish()
        g.wait_ge(T.sem.sent, sent[0])
        return

    def pass_on(a, b):
        piece = T.xin[:, a:b]
        return ([team[3 if k == 1 else 1], team[2]], piece, piece, on_chip, "xd2")
    if own:
        send("sxa", ["xa"], ([team[1]], T.xin[:, 0:XA], T.xin[:, 0:XA], half(on_chip, 0), "xd0"),
             ([team[3]], T.xin[:, XA:2 * XA], T.xin[:, XA:2 * XA], half(on_chip, 1), "xd0"))
    elif k == 1:
        send("fxa", ["xa"], pass_on(0, XA))
    elif k == 3:
        send("fxa", ["xa"], pass_on(XA, 2 * XA))

    if own:
        cp("kF", T.kF[:], T.kI[:], ["kI"])
        for u in range(8):
            mm("f0", T.f0[:, 0:16], T.zsel[:, 112 - 16 * u:240 - 16 * u], T.kF[:, u::8], u == 0, u == 7, ["zsel", "kF"])
        ts("hi1", T.hi[:, 0:16], T.f0[:, 0:16], -3.5, R8, OP.add, OP.add, rd=["f0"])
        ts("hi8", T.hi[:, 16:32], T.hi[:, 0:16], -R8, None, OP.add, rd=["hi1"])
        tt("lo", T.hi[:, 32:48], T.f0[:, 0:16], T.hi[:, 16:32], OP.subtract, ["f0", "hi8"])
        send("shi", ["hi8", "lo"], (team[1:], T.hi[:, 16:48], T.hi[:, 16:48], on_chip, "hs"))
        onehot("OHlo", T.OHlo, "Mm", T.Mm, T.hi[:, 32:48], 8, 128, 1, ["lo"])
        for t in range(NT):
            ts("OH%d" % (t // 4), tile("OH", t), T.iot8[:], T.hi[:, 16 + t:17 + t], None, OP.is_equal, rd=["hi8", "iot8"])
        for t in range(NT):
            mm("f2", T.f2[:, t:128:16], tile("OH", t), tile("OHlo", t, 8), True, True, ["OH%d" % (t // 4), "OHlo0"])
    else:
        for i in range(NL):
            t = 16 + NL * k + i
            ts("OH0", tile("OH", i), T.iot8[:], T.hi[:, t:t + 1], None, OP.is_equal, rd=["hi8", "iot8"])
        for l in range(8):
            t = 32 + NL * k
            ts("OHlo0", T.OHlo[:, l:8 * NL:8], T.hi[:, t:t + NL], float(l), None, OP.is_equal, rd=["hi8"])

    def transpose(i):
        out = tile("pT0", i)
        op("P", lambda: P.transpose(out, tile("OH", i), T.ident[:]), "pT0", ["OH0", "ident"])
    if own:
        scan("Ex", T.Ex[:, 1:129], T.ones[:], T.f2[:, 0:128], 0.0, ["f2", "ones"])
        for i in range(2):
            transpose(i)
        mm("f3", T.f3[:, 0:1], T.U4[:, 0:128], T.Ex[:, 128:129], True, True, ["U4", "Ex"])
        for i in range(2, NL):
            transpose(i)
        ts("A", T.At[:, 0:9], T.Ex[:, 0:129:16], T.f3[:, 0:1], None, OP.add, rd=["Ex", "Ex0", "f3", "hpad"])
        ts("St", T.St[:, 0:129], T.Ex[:, 0:129], T.f3[:, 0:1], None, OP.add, rd=["Ex", "Ex0", "f3"])
        table = tile("HA", r, 16)
        send("s0", ["A"], ([Z[x][0] for x in inr[r]], T.At[:], table, off_chip, "h1"), ([Z[r][0]], T.At[:], table, stay, "h1"))
        send("sst", ["St"], (team[1:], T.St[:, 0:128], T.St[:, 0:128], on_chip, "ss"))
        send("sxb", ["xb"], ([team[1]], T.xin[:, 2 * XA:XB], T.xin[:, 2 * XA:XB], half(on_chip, 0), "xd1"),
             ([team[3]], T.xin[:, XB:TC], T.xin[:, XB:TC], half(on_chip, 1), "xd1"))
    else:
        for i in range(NL):
            transpose(i)

    cp("OHT", T.OHT[:], T.pT0[:, 0:128 * NL], ["pT0"])
    for i in range(NL):
        mm("f4", tile("f4", i), tile("OHT", i), tile("OHT", i), True, True, ["OHT"])
    tt("Mm", T.Mm[:], T.f4[:, 0:128 * NL], T.U4[:, 0:128 * NL], OP.mult, ["f4", "U4"])
    for i in range(NL):
        o = tile("f2", i, 8)
        mm("f2", o, tile("OHT", i), T.St[:, NL * k + i:128:16], True, False, ["OHT", "St"])
        mm("f2", o, tile("Mm", i), tile("OHlo", i, 8), False, True, ["Mm", "OHlo0"])
    tt("prod", T.prod[:], T.f2[:, 0:8 * NL], T.OHlo[:, 0:8 * NL], OP.mult, ["f2", "OHlo0"])
    scan("SC", T.SC[:], T.rm8[:, 0:8 * NL], T.prod[:], 0.0, ["prod", "rm8"])
    ts("b1", T.Jd[:, 0:NL], T.SC[:, 7::8], -7.5, R16, OP.add, OP.add, rd=["SC"])
    ts("b0", T.Jd[:, NL:2 * NL], T.Jd[:, 0:NL], -R16, None, OP.add, rd=["b1"])
    for i in range(NL):
        key, b, t = "LA%d" % i, T.Jd[:, NL + i:NL + i + 1], NL * k + i
        ts(key, tile("LA", i), T.iom[:], b, T.SC[:, 8 * i + 7:8 * i + 8], OP.add, OP.is_equal, rd=[kc("iom"), "b0", "SC"])
        ts(key, tile("RB", i), T.iot16[:], b, jcol(t), OP.is_equal, OP.mult, rd=[kc("iot16"), kc("jcol"), "b0"])
    for i in range(NL):
        mm("f0", T.f0[:, 0:128], tile("LA", i), tile("RB", i), i == 0, i == NL - 1, ["LA%d" % i])
    mine_pl = tile("PL", k)
    cp("PL", mine_pl, T.f0[:, 0:128], ["f0"])
    send("spl", ["PL"], ([x for x in team if x != core], mine_pl, mine_pl, on_chip, "pl"))
    if k in (1, 3):
        send("fxb", ["xb"], pass_on(2 * XA, XB) if k == 1 else pass_on(XB, TC))

    places_of_runs()
    for l in range(8):
        e = 9 * l + r
        ts("Z", T.w32[:, l:56:8], Dd(7), T.G9[:, e:e + 1], T.HT[:, e + 1:e + 2], OP.subtract, OP.min, rd=[kc("Dd"), "G9", "HT"])
    ts("Zr", T.q3[:, 0:56], T.w32[:, 0:56], 0.0, None, OP.max, rd=["Z"])
    mm("f1", T.f1[:, 0:56], T.ones[:], T.q3[:, 0:56], True, True, ["ones", "Zr"])
    scan("SB", T.gb[:, 0:56], T.rm8[:], T.f1[:, 0:56], 0.0, ["f1", "rm8"])
    ts("be0", T.be0[:, 0:7], T.gb[:, 7:56:8], -7.5, R16, OP.add, OP.add, rd=["SB"])
    ts("be", T.be[:, 1:8], T.be0[:, 0:7], -R16, 0.0625, OP.add, OP.mult, rd=["be0"])
    x0, x1, x2 = inr[r]
    w0, w1, w2 = [cab[q] for q in inr[r]]
    blocks = ((c, x2, r), (w0, x0), (w1,), (w2, x1))[k]
    for i, d in enumerate(blocks):
        ts("sh%d" % i, T.sh[:, 4 * i:4 * i + 3], lin(3), T.be[:, d:d + 1], None, OP.add, rd=[kc("lin"), "be", "be_0"])
    for i in range(K):
        mm("f3", T.f3[:, 0:128], T.ident[:], tile("PL", i), i == 0, i == K - 1, ["ident", "PL" if i == k else "PLx"])
    cp("invF", T.invF[:, 0:128], T.f3[:, 0:128], ["f3"])

    def cut(i):
        cp("off%d" % i, T.off[:, SW * i:SW * i + SW], T.invF[:].indirect(T.sh[:, 4 * i:4 * i + 3]), ["invF", "invP", "sh%d" % i])

    def gather(f, i, a, b):
        o = BLK * (lp(r) if blocks[i] == r else i)
        f("st%d_%d" % (i, a), T["land" if blocks[i] == r else "stage"][:, o + a:o + b],
          T.xin[:].indirect(T.off[:, SW * i + a // 16:SW * i + b // 16]), xr + ["off%d" % i])

    def ship(i, a, b, keys, sem):
        d = blocks[i]
        to = W[(r, d)] if (r, d) in W else cores[d]
        o = 0 if (r, d) in W else BLK * lp(r)
        send("sb%d_%d" % (i, a), ["st%d_%d" % (i, z) for z in keys],
             ([to], T.stage[:, BLK * i + a:BLK * i + b], T.land[:, o + a:o + b], off_chip, sem))
    for i, d in enumerate(blocks):
        cut(i)
        if (r, d) in W:
            for f, (a, b) in zip((act, cp), PARTS):
                gather(f, i, a, b)
            for q, (a, b) in enumerate(PARTS):
                ship(i, a, b, [a], "rel%d" % q)
        else:
            gather(cp, i, 0, M)
            gather(act, i, M, BLK)
            if d != r:
                ship(i, 0, BLK, [0, M], "dat")
    if not own:
        finish()
        g.wait_ge(T.sem.sent, sent[0])
        return

    tt("yl32", T.Rr[:], T.ylp[:, 0:128], T.ylp[:, 128:256], OP.add, ["ylp"])
    cp("yl", T.yl[:], T.Rr[:], ["yl32"])
    for q in range(4):
        (cp if q % 2 == 0 else act)("y%d" % q, T.yout[:, YC[q]:YC[q + 1]], T.land[:].indirect(T.yl[:, YC[q] // 16:YC[q + 1] // 16]),
                                    ["yl", "dat", "st2_0", "st2_%d" % M])
    for q in range(4):
        dma("yo", T.y[:, YC[q]:YC[q + 1]], T.yout[:, YC[q]:YC[q + 1]], ["y%d" % q])
    op("Y", lambda: None, "end", ["yo"], 0)
    finish()
    g.wait_ge(T.sem.sent, sent[0])


def make_list(r, zi, T, calls, tile, w32):
    mm, ts, tt, scan, cp, onehot = calls
    ss = list(range(N // 2 * zi, N // 2 * zi + N // 2))
    al, pb, ga = T.SC[:, 0:8], T.prod[:, 0:1], T.LA[:, 0:72]
    ts("q1", w32(0), T.G9[:], -1.0, float(TC * r), OP.mult, OP.add, rd=["G9"])
    ts("gp", T.gp[:, 144:216], T.G9[:], float(TC * r), 0.0, OP.subtract, OP.max, rd=["G9"])
    tt("q2", w32(1, 0, 71), w32(0, 0, 71), T.HT[:, 1:72], OP.min, ["q1", "HT", "HT0"])
    ts("gab32", T.gp[:, 0:72], T.gp[:, 144:216], 15, None, OP.bitwise_and, rd=["gp"])
    ts("gab32", T.gp[:, 72:144], T.gp[:, 144:216], 4, None, OP.arith_shift_right, rd=["gp"])
    ts("q3", T.q3[:, 0:71], w32(1, 0, 71), 0.0, None, OP.max, rd=["q2"])
    for l in range(8):
        mm("f3", T.f3[:, 0:8], T.ones[:], T.q3[:, 9 * l:9 * l + 8], l == 0, l == 7, ["ones", "q3"])
    cp("ga", ga, T.gp[:, 0:72], ["gab32"])
    cp("gb", T.gb[:], T.gp[:, 72:144], ["gab32"])
    onehot("LS", T.LS, "apart", T.stage, ga, 16, 1152, 4, ["ga"])
    ts("be0", T.be0[:], T.f3[:, 0:8], -7.5, R16, OP.add, OP.add, rd=["f3"])
    for s in [(ss[0] - 1) % N] + ss:
        ts("a1", w32(2, 9 * s, 9 * s + 9), T.HA[:, 16 * s:16 * s + 9], T.f3[:, s:s + 1], 0.0, OP.subtract, OP.max,
           rd=["f3", "h2", "h3"])
    ts("be", T.be[:], T.be0[:], -R16, None, OP.add, rd=["be0"])
    lo, hi = 9 * ss[0], 9 * ss[-1] + 9
    for a, b in ((lo - 9, hi),) if zi else ((lo, hi), (63, 72)):
        ts("a2", w32(3, a, b), w32(2, a, b), float(CAPP), None, OP.min, rd=["a1"])
    tt("al", al, T.f3[:, 0:8], T.be[:], OP.subtract, ["f3", "be"])
    if zi:
        tt("dl", w32(4, lo, hi), w32(3, lo, hi), w32(3, lo - 8, hi - 8), OP.subtract, ["a2"])
    else:
        tt("dl", w32(4, 9, hi), w32(3, 9, hi), w32(3, 1, hi - 8), OP.subtract, ["a2"])
        tt("dl", w32(4, 0, 8), w32(3, 0, 8), w32(3, 63, 71), OP.subtract, ["a2"])
    tt("Jd", T.Jd[:, 1:8], T.SC[:, 1:8], T.SC[:, 0:7], OP.subtract, ["al"])
    tt("Jd", T.Jd[:, 0:1], T.SC[:, 0:1], T.SC[:, 7:8], OP.subtract, ["al"])
    if zi:
        ts("pb", pb, T.pa[:, 0:1], T.SC[:, 7:8], None, OP.add, rd=["pa", "al"])
    for s in ss:
        ts("dl2", w32(5, 9 * s, 9 * s + 8), w32(4, 9 * s, 9 * s + 8), T.Jd[:, s:s + 1], float(BLK * (lp(s) - lp((s - 1) % N))),
           OP.add, OP.add, rd=["dl", "Jd"])
    runs = [(l, s) for l in range(8) for s in ss]
    n = len(runs)
    for i, (l, s) in enumerate(runs):
        e = 9 * l + s
        ts("sg%d" % (i // 4), tile("RS", i), T.iot[:, 0:128], T.gb[:, e:e + 1], w32(5, 9 * s + l, 9 * s + l + 1), OP.is_equal, OP.mult,
           rd=["iot", "gb", "dl2"])
    for i, (l, s) in enumerate(runs):
        mm("f4", T.f4[:, 0:16], tile("RS", i), tile("LS", 9 * l + s, 16), i == 0, i == n - 1, ["sg%d" % (i // 4), "LS%d" % (l // 2)])
    scan("E", T.E[:], T.ones[:, 0:16], T.f4[:, 0:16], 0.0, ["f4", "ones"])
    ts("Rr", T.Rr[:], T.ones[:], T.E[:, 15:16], 16.0 * zi, OP.mult, OP.add, rd=["E", "ones"])
    mm("f2", T.f2[:, 0:128], T.Rr[:], T.U32[:], True, False, ["Rr", "U32"])
    cp("Er", T.Er[:], T.E[:].indirect(T.sh[:, 0:8]), ["E", "rep"])
    mm("f2", T.f2[:, 0:128], T.Er[:], T.id32[:], False, True, ["Er", "id32"])
    if zi:
        ts("ylp", tile("ylp", zi), T.f2[:, 0:128], pb, None, OP.add, rd=["f2", "pb"])
    else:
        cp("ylp", tile("ylp", zi), T.f2[:, 0:128], ["f2"])


def helper(g, core, T, topo, job, cores):
    s, d = job
    rid, pid = topo.addr(cores[d], core)
    m = topo.mask(core, cores[d])

    def relay(q):
        a, b = PARTS[q]
        o = BLK * lp(s)
        return g.remote_dma(T.land[:, o + a:o + b], T.land[:, a:b], T.sem.dat, T.sem.sent, pid, rid, m)
    return count_bits(m), relay
